import numpy as np
import ml_dtypes


def mxq(x, axis, fmt="e4m3"):
    dtype, down = {"e4m3": (ml_dtypes.float8_e4m3fn, 7), "e5m2": (ml_dtypes.float8_e5m2, 14)}[fmt]
    v = np.moveaxis(np.asarray(x, np.float32).astype(ml_dtypes.bfloat16).astype(np.float64), axis, -1)
    blocks = v.reshape(v.shape[:-1] + (-1, 32))
    amax = np.abs(blocks).max(-1, keepdims=True)
    byte = np.maximum(np.where(amax > 0, np.frexp(amax)[1] - 1 + 127, 0) - down, 1)
    scale = np.exp2(byte - 127.0)
    codes = (blocks / scale).astype(np.float32).astype(dtype).astype(np.float64)
    return np.moveaxis((codes * scale).reshape(v.shape), -1, axis)


WIDE = False


def mx_kscale(k):
    if not WIDE:
        return np.ones(k)
    levels = np.array([10, -10, 5, -5, 0])
    if k % 512:
        return np.exp2(np.random.permutation(np.resize(levels, k // 32))).repeat(32)
    a = np.empty((k // 512, 16))
    for p in range(k // 512):
        a[p, :8] = np.random.permutation(np.resize(levels, 8))
        for g in range(8):
            far = levels[np.abs(levels - a[p, g]) >= 10]
            a[p, g + 8] = far[np.random.randint(len(far))]
    return np.exp2(a.ravel()).repeat(32)


def f64(x):
    return np.asarray(x).astype(np.float64)


def striped(idx):
    return np.tile(idx.reshape(-1, 16).T, (8, 1)).astype(np.uint16)


def unstriped(offs):
    return offs[:16].T.reshape(-1).astype(np.int64)


E2M1 = np.array([0.0, 0.5, 1.0, 1.5, 2.0, 3.0, 4.0, 6.0, -0.0, -0.5, -1.0, -1.5, -2.0, -3.0, -4.0, -6.0])


def pack_weight(w, fmt):
    k, n = w.shape
    w = f64(np.asarray(w, np.float32).astype(ml_dtypes.bfloat16)).reshape(k // 32, 32, n)
    amax = np.abs(w).max(1)
    if fmt == "e4m3":
        byte = np.frexp(amax)[1] - 1 + 127 - 7
    else:
        mant, ex = np.frexp(amax / 6.0)
        byte = np.where(mant > 0.5, ex, ex - 1) + 127
    byte = np.clip(np.where(amax > 0, byte, 1), 1, 254)
    scaled = (w * np.exp2(127.0 - byte)[:, None, :]).reshape(k, n).astype(np.float32)
    by_word = np.ascontiguousarray(scaled.reshape(k // 512, 128, 4, n).transpose(0, 1, 3, 2))
    if fmt == "e4m3":
        words = by_word.astype(ml_dtypes.float8_e4m3fn).view(np.uint8)
    else:
        c = by_word.astype(ml_dtypes.float4_e2m1fn).view(np.uint8) & 0xF
        words = (c[..., 0::2] | (c[..., 1::2] << 4)).reshape(k // 512, 128, 2 * n)
    return np.ascontiguousarray(words), np.ascontiguousarray(byte.astype(np.uint8).reshape(k // 512, 16, n))


def unpack_weight(words, scales, fmt):
    g, _, n = scales.shape
    words = np.ascontiguousarray(words).reshape(g, 128, n, -1)
    if fmt == "e4m3":
        vals = words.view(ml_dtypes.float8_e4m3fn).astype(np.float64)
    else:
        nib = np.empty((g, 128, n, 4), np.uint8)
        nib[..., 0::2] = words & 0xF
        nib[..., 1::2] = words >> 4
        vals = E2M1[nib]
    vals = vals * np.repeat(np.exp2(scales.astype(np.float64) - 127.0), 8, axis=1)[..., None]
    return vals.transpose(0, 1, 3, 2).reshape(g * 512, n)


def pack_table(v):
    words, scales = pack_weight(v, "e4m3")
    return np.concatenate([words.reshape(words.shape[0], -1), scales.reshape(scales.shape[0], -1)], axis=1)


def unpack_table(tab):
    g, t = tab.shape[0], tab.shape[1] // 528
    return unpack_weight(tab[:, :512 * t].reshape(g, 128, t, 4), tab[:, 512 * t:].reshape(g, 16, t), "e4m3")


K, H, M, T, S = 512, 512, 1024, 2048, 512


def setup_inputs():
    n = np.random.standard_normal
    s = mx_kscale(K)[:, None]
    u = mx_kscale(H)[:, None]
    p_w2 = pack_weight(1.4 * n((H, M)) / np.sqrt(H) / u, "e2m1")
    return {
        "tab": pack_table(n((K, T)) * s),
        "w1": (n((K, H)) / np.sqrt(K) / s * u.T).astype(np.float32),
        "w2_words": p_w2[0],
        "w2_scales": p_w2[1],
        "b": (0.3 * n(1024)).astype(np.float32),
        "offs": striped(np.random.permutation(T)[:S]),
    }


def reference(tab, w1, w2_words, w2_scales, b, offs):
    tab_ = unpack_table(tab)[:, unstriped(offs)]
    w1_ = mxq(f64(w1), 0, "e4m3")
    w2_ = unpack_weight(w2_words, w2_scales, "e2m1")
    h_ = mxq(np.maximum(w1_.T @ tab_, 0.0), 0, "e4m3")
    y = h_.T @ w2_
    return y + f64(b)[None, :]

@@ -1,0 +1,163 @@
+from contextlib import ExitStack
+
+import concourse.mybir as mybir
+from concourse.masks import make_identity
+
+K, H, M, T, S = 512, 512, 1024, 2048, 512
+FLOPS = 2 * K * H * S + 2 * H * M * S
+
+P = 128
+F32 = mybir.dt.float32
+BF16 = mybir.dt.bfloat16
+I32 = mybir.dt.int32
+U32 = mybir.dt.uint32
+U16 = mybir.dt.uint16
+U8 = mybir.dt.uint8
+FP8X4 = mybir.dt.float8_e4m3fn_x4
+FP4X4 = mybir.dt.float4_e2m1fn_x4
+COPY = mybir.ActivationFunctionType.Copy
+RELU = mybir.ActivationFunctionType.Relu
+ADD = mybir.AluOpType.add
+
+W1_VECTOR = 64
+
+
+def tile_list_tabmlp_tm_bias_kernel(tc, tab, w1, w2_words, w2_scales, b, offs, out):
+    nc = tc.nc
+    with ExitStack() as ctx:
+        keep = ctx.enter_context(tc.tile_pool(name="keep", bufs=1))
+        ring = ctx.enter_context(tc.tile_pool(name="ring", bufs=4))
+        outs = ctx.enter_context(tc.tile_pool(name="outs", bufs=9))
+        psum = ctx.enter_context(tc.psum_pool(name="psum", bufs=8))
+
+        offsets = keep.tile([P, S // 16], U16, name="offsets")
+        b_col = keep.tile([P, 8], F32, name="b_col")
+        tab_words = keep.tile([P, T], U32, name="tab_words", align_bytes=64)
+        tab_scales = keep.tile([P, T], U8, name="tab_scales", align_bytes=64)
+        w1_raw = keep.tile([P, 4, H], F32, name="w1_raw", align_bytes=64)
+        w2_codes = keep.tile([P, 2 * M], U8, name="w2_codes", align_bytes=64)
+        w2_sc = keep.tile([P, M], U8, name="w2_sc", align_bytes=64)
+
+        nc.vector.memset(tab_scales[:].bitcast(I32), 0)
+        nc.gpsimd.memset(w2_sc[:].bitcast(I32), 0)
+
+        nc.sync.dma_start(offsets[:], offs)
+        nc.scalar.dma_start(out=b_col[:], in_=b.rearrange("(n c) -> n c", c=8))
+        nc.sync.dma_start(out=w1_raw[:], in_=w1.rearrange("(p j) r -> p j r", j=4))
+        scales_dram = tab[0, 512 * T : 528 * T].rearrange("(q t) -> q t", q=16)
+        for q in range(4):
+            nc.sync.dma_start(
+                out=tab_scales[32 * q : 32 * q + 4, :].bitcast(I32),
+                in_=scales_dram[4 * q : 4 * q + 4, :].bitcast(I32),
+            )
+        words_dram = tab[0, 0 : 512 * T].rearrange("(p b) -> p b", p=P)
+        nc.sync.dma_start(out=tab_words[:].bitcast(I32), in_=words_dram.bitcast(I32))
+        nc.sync.dma_start(out=w2_codes[:].bitcast(I32), in_=w2_words[0].bitcast(I32))
+        for q in range(4):
+            nc.sync.dma_start(
+                out=w2_sc[32 * q : 32 * q + 4, :].bitcast(I32),
+                in_=w2_scales[0, 4 * q : 4 * q + 4, :].bitcast(I32),
+            )
+
+        ident = keep.tile([P, P], F32, name="ident")
+        make_identity(nc, ident[:])
+        bias = keep.tile([P, M], F32, name="bias")
+        bias_v = bias[:].rearrange("p (n u c) -> p u n c", u=2, c=4)
+        for u in range(2):
+            bank = psum.tile([P, 512], F32, name="bank")
+            for c in range(4):
+                column = b_col[:, 4 * u + c : 4 * u + c + 1].to_broadcast([P, P])
+                nc.tensor.transpose(bank[:, 128 * c : 128 * c + 128], column, ident[:])
+            nc.scalar.activation(bias_v[:, u], bank[:].rearrange("p (c n) -> p n c", c=4), COPY)
+
+        x_scales = []
+
+        def gather_scales(g):
+            scales = keep.tile([P, 256], U8, name=f"x_scales{g}", align_bytes=64)
+            nc.vector.tensor_copy(scales[:], tab_scales[:].indirect(offsets[:, 16 * g : 16 * g + 16]))
+            x_scales.append(scales)
+
+        w1_bf = keep.tile([P, 4 * H], BF16, name="w1_bf", align_bytes=64)
+        w1_dst = w1_bf[:].rearrange("p (t m j) -> p m t j", t=4, j=4)
+        w1_src = w1_raw[:].rearrange("p j (m t) -> p m t j", t=4)
+        nc.vector.tensor_copy(out=w1_dst[:, :W1_VECTOR], in_=w1_src[:, :W1_VECTOR])
+        nc.scalar.activation(w1_dst[:, W1_VECTOR:], w1_src[:, W1_VECTOR:], COPY)
+        w1_codes = keep.tile([P, H], U32, name="w1_codes", align_bytes=64)
+        w1_sc = keep.tile([P, H], U8, name="w1_sc", align_bytes=64)
+        gather_scales(0)
+        nc.vector.quantize_mx(out=w1_codes[:].bitcast(FP8X4), scales=w1_sc[:], in_=w1_bf[:])
+
+        x_words = []
+        for g in range(2):
+            words = keep.tile([P, 256], U32, name=f"x_words{g}", align_bytes=64)
+            nc.vector.tensor_copy(words[:], tab_words[:].indirect(offsets[:, 16 * g : 16 * g + 16]))
+            x_words.append(words)
+
+        gather_scales(1)
+
+        h_banks, h_codes = [], []
+
+        def first_product(c):
+            bank = psum.tile([P, 512], F32, name="bank")
+            cols = slice(128 * (c % 2), 128 * (c % 2) + 128)
+            for t in range(4):
+                r = slice(128 * t, 128 * t + 128)
+                nc.tensor.matmul_mx(
+                    out=bank[:, r],
+                    lhsT=w1_codes[:, r].bitcast(FP8X4),
+                    lhsT_scale=w1_sc[:, r],
+                    rhs=x_words[c // 2][:, cols].bitcast(FP8X4),
+                    rhs_scale=x_scales[c // 2][:, cols],
+                    start=True,
+                    stop=True,
+                )
+            h_bf = ring.tile([P, 512], BF16, name="h_bf", align_bytes=64)
+            nc.scalar.activation(
+                h_bf[:].rearrange("p (n t) -> p n t", t=4), bank[:].rearrange("p (t n) -> p n t", t=4), RELU
+            )
+            h_banks.append(h_bf)
+
+        def quantise(c):
+            codes = ring.tile([P, 128], U32, name="h_codes", align_bytes=64)
+            scales = ring.tile([P, 128], U8, name="h_scales", align_bytes=64)
+            nc.vector.quantize_mx(out=codes[:].bitcast(FP8X4), scales=scales[:], in_=h_banks[c][:])
+            h_codes.append((codes, scales))
+
+        def second_product(c, n0, width, on_gpsimd=False):
+            codes, scales = h_codes[c]
+            bank = psum.tile([P, 512], F32, name="bank")
+            cols = slice(n0, n0 + width)
+            nc.tensor.matmul_mx(
+                out=bank[:, :width],
+                lhsT=codes[:].bitcast(FP8X4),
+                lhsT_scale=scales[:],
+                rhs=w2_codes[:, 2 * n0 : 2 * (n0 + width)].bitcast(FP4X4),
+                rhs_scale=w2_sc[:, cols],
+                start=True,
+                stop=True,
+            )
+            result = outs.tile([P, 512], F32, name="result")
+            if on_gpsimd:
+                nc.scalar.activation(result[:, :width], bank[:, :width], COPY)
+                nc.gpsimd.tensor_tensor(result[:, :width], result[:, :width], bias[:, cols], ADD)
+            else:
+                nc.vector.tensor_tensor(result[:, :width], bank[:, :width], bias[:, cols], ADD)
+            nc.sync.dma_start(out=out[128 * c : 128 * c + 128, cols], in_=result[:, :width])
+
+        first_product(0)
+        first_product(1)
+        quantise(0)
+        second_product(0, 0, 256)
+        second_product(0, 256, 256)
+        first_product(2)
+        quantise(1)
+        second_product(0, 512, 512, on_gpsimd=True)
+        first_product(3)
+        second_product(1, 0, 512)
+        quantise(2)
+        second_product(1, 512, 512)
+        second_product(2, 0, 512)
+        quantise(3)
+        second_product(2, 512, 512, on_gpsimd=True)
+        second_product(3, 0, 512)
+        second_product(3, 512, 512)

@@ -27,8 +27,9 @@ def tile_list_tabmlp_tm_bias_kernel(tc, tab, w1, w2_words, w2_scales, b, offs, o
     with ExitStack() as ctx:
         keep = ctx.enter_context(tc.tile_pool(name="keep", bufs=1))
         ring = ctx.enter_context(tc.tile_pool(name="ring", bufs=4))
-        outs = ctx.enter_context(tc.tile_pool(name="outs", bufs=9))
-        psum = ctx.enter_context(tc.psum_pool(name="psum", bufs=8))
+        outs = ctx.enter_context(tc.tile_pool(name="outs", bufs=10))
+        h_psum = ctx.enter_context(tc.psum_pool(name="h_psum", bufs=1))
+        y_psum = ctx.enter_context(tc.psum_pool(name="y_psum", bufs=4))
 
         offsets = keep.tile([P, S // 16], U16, name="offsets")
         b_col = keep.tile([P, 8], F32, name="b_col")
@@ -37,6 +38,8 @@ def tile_list_tabmlp_tm_bias_kernel(tc, tab, w1, w2_words, w2_scales, b, offs, o
         w1_raw = keep.tile([P, 4, H], F32, name="w1_raw", align_bytes=64)
         w2_codes = keep.tile([P, 2 * M], U8, name="w2_codes", align_bytes=64)
         w2_sc = keep.tile([P, M], U8, name="w2_sc", align_bytes=64)
+        scales_dram = tab[0, 512 * T : 528 * T].rearrange("(q t) -> q t", q=16)
+        words_dram = tab[0, 0 : 512 * T].rearrange("(p b) -> p b", p=P)
 
         nc.vector.memset(tab_scales[:].bitcast(I32), 0)
         nc.gpsimd.memset(w2_sc[:].bitcast(I32), 0)
@@ -44,47 +47,33 @@ def tile_list_tabmlp_tm_bias_kernel(tc, tab, w1, w2_words, w2_scales, b, offs, o
         nc.sync.dma_start(offsets[:], offs)
         nc.scalar.dma_start(out=b_col[:], in_=b.rearrange("(n c) -> n c", c=8))
         nc.sync.dma_start(out=w1_raw[:], in_=w1.rearrange("(p j) r -> p j r", j=4))
-        scales_dram = tab[0, 512 * T : 528 * T].rearrange("(q t) -> q t", q=16)
-        for q in range(4):
-            nc.sync.dma_start(
-                out=tab_scales[32 * q : 32 * q + 4, :].bitcast(I32),
-                in_=scales_dram[4 * q : 4 * q + 4, :].bitcast(I32),
-            )
-        words_dram = tab[0, 0 : 512 * T].rearrange("(p b) -> p b", p=P)
+        for r in range(4):
+            nc.sync.dma_start(out=tab_scales[r:P:32, :].bitcast(I32), in_=scales_dram[r:16:4, :].bitcast(I32))
         nc.sync.dma_start(out=tab_words[:].bitcast(I32), in_=words_dram.bitcast(I32))
         nc.sync.dma_start(out=w2_codes[:].bitcast(I32), in_=w2_words[0].bitcast(I32))
-        for q in range(4):
-            nc.sync.dma_start(
-                out=w2_sc[32 * q : 32 * q + 4, :].bitcast(I32),
-                in_=w2_scales[0, 4 * q : 4 * q + 4, :].bitcast(I32),
-            )
+        for r in range(4):
+            nc.sync.dma_start(out=w2_sc[r:P:32, :].bitcast(I32), in_=w2_scales[0, r:16:4, :].bitcast(I32))
 
         ident = keep.tile([P, P], F32, name="ident")
         make_identity(nc, ident[:])
         bias = keep.tile([P, M], F32, name="bias")
         bias_v = bias[:].rearrange("p (n u c) -> p u n c", u=2, c=4)
         for u in range(2):
-            bank = psum.tile([P, 512], F32, name="bank")
+            bank = y_psum.tile([P, 512], F32, name="y_bank")
             for c in range(4):
                 column = b_col[:, 4 * u + c : 4 * u + c + 1].to_broadcast([P, P])
                 nc.tensor.transpose(bank[:, 128 * c : 128 * c + 128], column, ident[:])
             nc.scalar.activation(bias_v[:, u], bank[:].rearrange("p (c n) -> p n c", c=4), COPY)
-
-        x_scales = []
-
-        def gather_scales(g):
-            scales = keep.tile([P, 256], U8, name=f"x_scales{g}", align_bytes=64)
-            nc.vector.tensor_copy(scales[:], tab_scales[:].indirect(offsets[:, 16 * g : 16 * g + 16]))
-            x_scales.append(scales)
 
         w1_bf = keep.tile([P, 4 * H], BF16, name="w1_bf", align_bytes=64)
         w1_dst = w1_bf[:].rearrange("p (t m j) -> p m t j", t=4, j=4)
         w1_src = w1_raw[:].rearrange("p j (m t) -> p m t j", t=4)
         nc.vector.tensor_copy(out=w1_dst[:, :W1_VECTOR], in_=w1_src[:, :W1_VECTOR])
         nc.scalar.activation(w1_dst[:, W1_VECTOR:], w1_src[:, W1_VECTOR:], COPY)
+        x_scales = keep.tile([P, S], U8, name="x_scales", align_bytes=64)
+        nc.vector.tensor_copy(x_scales[:], tab_scales[:].indirect(offsets[:]))
         w1_codes = keep.tile([P, H], U32, name="w1_codes", align_bytes=64)
         w1_sc = keep.tile([P, H], U8, name="w1_sc", align_bytes=64)
-        gather_scales(0)
         nc.vector.quantize_mx(out=w1_codes[:].bitcast(FP8X4), scales=w1_sc[:], in_=w1_bf[:])
 
         x_words = []
@@ -93,12 +82,10 @@ def tile_list_tabmlp_tm_bias_kernel(tc, tab, w1, w2_words, w2_scales, b, offs, o
             nc.vector.tensor_copy(words[:], tab_words[:].indirect(offsets[:, 16 * g : 16 * g + 16]))
             x_words.append(words)
 
-        gather_scales(1)
+        h_rounded, h_codes = [], []
 
-        h_banks, h_codes = [], []
-
-        def first_product(c):
-            bank = psum.tile([P, 512], F32, name="bank")
+        def first_product(c, tag):
+            bank = h_psum.tile([P, 512], F32, name=tag)
             cols = slice(128 * (c % 2), 128 * (c % 2) + 128)
             for t in range(4):
                 r = slice(128 * t, 128 * t + 128)
@@ -107,7 +94,7 @@ def tile_list_tabmlp_tm_bias_kernel(tc, tab, w1, w2_words, w2_scales, b, offs, o
                     lhsT=w1_codes[:, r].bitcast(FP8X4),
                     lhsT_scale=w1_sc[:, r],
                     rhs=x_words[c // 2][:, cols].bitcast(FP8X4),
-                    rhs_scale=x_scales[c // 2][:, cols],
+                    rhs_scale=x_scales[:, 128 * c : 128 * c + 128],
                     start=True,
                     stop=True,
                 )
@@ -115,49 +102,52 @@ def tile_list_tabmlp_tm_bias_kernel(tc, tab, w1, w2_words, w2_scales, b, offs, o
             nc.scalar.activation(
                 h_bf[:].rearrange("p (n t) -> p n t", t=4), bank[:].rearrange("p (t n) -> p n t", t=4), RELU
             )
-            h_banks.append(h_bf)
+            h_rounded.append(h_bf)
 
         def quantise(c):
             codes = ring.tile([P, 128], U32, name="h_codes", align_bytes=64)
             scales = ring.tile([P, 128], U8, name="h_scales", align_bytes=64)
-            nc.vector.quantize_mx(out=codes[:].bitcast(FP8X4), scales=scales[:], in_=h_banks[c][:])
+            nc.vector.quantize_mx(out=codes[:].bitcast(FP8X4), scales=scales[:], in_=h_rounded[c][:])
             h_codes.append((codes, scales))
 
-        def second_product(c, n0, width, on_gpsimd=False):
+        def product(c, n0, width, tag):
             codes, scales = h_codes[c]
-            bank = psum.tile([P, 512], F32, name="bank")
-            cols = slice(n0, n0 + width)
+            pool = y_psum if tag == "y_bank" else h_psum
+            bank = pool.tile([P, 512], F32, name=tag)
             nc.tensor.matmul_mx(
                 out=bank[:, :width],
                 lhsT=codes[:].bitcast(FP8X4),
                 lhsT_scale=scales[:],
                 rhs=w2_codes[:, 2 * n0 : 2 * (n0 + width)].bitcast(FP4X4),
-                rhs_scale=w2_sc[:, cols],
+                rhs_scale=w2_sc[:, n0 : n0 + width],
                 start=True,
                 stop=True,
             )
-            result = outs.tile([P, 512], F32, name="result")
-            if on_gpsimd:
-                nc.scalar.activation(result[:, :width], bank[:, :width], COPY)
-                nc.gpsimd.tensor_tensor(result[:, :width], result[:, :width], bias[:, cols], ADD)
-            else:
-                nc.vector.tensor_tensor(result[:, :width], bank[:, :width], bias[:, cols], ADD)
-            nc.sync.dma_start(out=out[128 * c : 128 * c + 128, cols], in_=result[:, :width])
+            return bank
 
-        first_product(0)
-        first_product(1)
+        def second_product(c, n0, width, pieces=1, tag="y_bank"):
+            bank = product(c, n0, width, tag)
+            step = width // pieces
+            for i in range(pieces):
+                cols = slice(n0 + i * step, n0 + (i + 1) * step)
+                result = outs.tile([P, 512], F32, name="result")
+                nc.vector.tensor_tensor(result[:, :step], bank[:, i * step : (i + 1) * step], bias[:, cols], ADD)
+                nc.sync.dma_start(out=out[128 * c : 128 * c + 128, cols], in_=result[:, :step])
+
+        first_product(0, "h0")
+        first_product(1, "h1")
+        first_product(2, "h2")
         quantise(0)
-        second_product(0, 0, 256)
+        second_product(0, 0, 256, tag="h3")
         second_product(0, 256, 256)
-        first_product(2)
+        first_product(3, "h3")
         quantise(1)
-        second_product(0, 512, 512, on_gpsimd=True)
-        first_product(3)
-        second_product(1, 0, 512)
+        second_product(0, 512, 512)
         quantise(2)
+        second_product(1, 0, 512)
+        quantise(3)
         second_product(1, 512, 512)
         second_product(2, 0, 512)
-        quantise(3)
-        second_product(2, 512, 512, on_gpsimd=True)
+        second_product(2, 512, 512)
         second_product(3, 0, 512)
-        second_product(3, 512, 512)
+        second_product(3, 512, 512, pieces=2)

@@ -19,13 +19,12 @@ COPY = mybir.ActivationFunctionType.Copy
 RELU = mybir.ActivationFunctionType.Relu
 ADD = mybir.AluOpType.add
 
-W1_VECTOR = 64
-
 
 def tile_list_tabmlp_tm_bias_kernel(tc, tab, w1, w2_words, w2_scales, b, offs, out):
     nc = tc.nc
     with ExitStack() as ctx:
         keep = ctx.enter_context(tc.tile_pool(name="keep", bufs=1))
+        shared = ctx.enter_context(tc.tile_pool(name="shared", bufs=1))
         ring = ctx.enter_context(tc.tile_pool(name="ring", bufs=4))
         outs = ctx.enter_context(tc.tile_pool(name="outs", bufs=10))
         h_psum = ctx.enter_context(tc.psum_pool(name="h_psum", bufs=1))
@@ -34,47 +33,58 @@ def tile_list_tabmlp_tm_bias_kernel(tc, tab, w1, w2_words, w2_scales, b, offs, o
         offsets = keep.tile([P, S // 16], U16, name="offsets")
         b_col = keep.tile([P, 8], F32, name="b_col")
         tab_words = keep.tile([P, T], U32, name="tab_words", align_bytes=64)
-        tab_scales = keep.tile([P, T], U8, name="tab_scales", align_bytes=64)
-        w1_raw = keep.tile([P, 4, H], F32, name="w1_raw", align_bytes=64)
-        w2_codes = keep.tile([P, 2 * M], U8, name="w2_codes", align_bytes=64)
-        w2_sc = keep.tile([P, M], U8, name="w2_sc", align_bytes=64)
+        tab_scales = shared.tile([P, T], U8, name="tab_scales", align_bytes=64, offset=0)
+        w1_low = keep.tile([P, 4, H // 2], F32, name="w1_low", tag="w1_low", align_bytes=64)
+        w1_high = keep.tile([P, 4, H // 2], F32, name="w1_high", align_bytes=64)
         scales_dram = tab[0, 512 * T : 528 * T].rearrange("(q t) -> q t", q=16)
         words_dram = tab[0, 0 : 512 * T].rearrange("(p b) -> p b", p=P)
 
+        gathered_scales = keep.tile([P, S], U8, name="gathered_scales", align_bytes=64)
+        x_scales = keep.tile([P, S], U8, name="x_scales", align_bytes=64)
         nc.vector.memset(tab_scales[:].bitcast(I32), 0)
-        nc.gpsimd.memset(w2_sc[:].bitcast(I32), 0)
+        nc.vector.memset(x_scales[:].bitcast(I32), 0)
 
+        w1_rows = w1.rearrange("(p j) r -> p j r", j=4)
+        nc.sync.dma_start(out=w1_low[:], in_=w1_rows[:, :, : H // 2])
         nc.sync.dma_start(offsets[:], offs)
-        nc.scalar.dma_start(out=b_col[:], in_=b.rearrange("(n c) -> n c", c=8))
-        nc.sync.dma_start(out=w1_raw[:], in_=w1.rearrange("(p j) r -> p j r", j=4))
-        for r in range(4):
-            nc.sync.dma_start(out=tab_scales[r:P:32, :].bitcast(I32), in_=scales_dram[r:16:4, :].bitcast(I32))
+        nc.sync.dma_start(out=b_col[:], in_=b.rearrange("(n c) -> n c", c=8))
+        nc.sync.dma_start(out=tab_scales[0:P:8, :].bitcast(I32), in_=scales_dram.bitcast(I32))
+        nc.sync.dma_start(out=w1_high[:], in_=w1_rows[:, :, H // 2 :])
         nc.sync.dma_start(out=tab_words[:].bitcast(I32), in_=words_dram.bitcast(I32))
+        nc.vector.tensor_copy(gathered_scales[:], tab_scales[:].indirect(offsets[:]))
+        for r in range(4):
+            nc.sync.dma_start(
+                out=x_scales[r:P:32, :].bitcast(I32), in_=gathered_scales[8 * r : P : 32, :].bitcast(I32)
+            )
+        w2_codes = shared.tile([P, 2 * M], U8, name="w2_codes", align_bytes=64, offset=M)
+        w2_sc = shared.tile([P, M], U8, name="w2_sc", align_bytes=64, offset=0)
+        nc.gpsimd.memset(w2_sc[:].bitcast(I32), 0)
         nc.sync.dma_start(out=w2_codes[:].bitcast(I32), in_=w2_words[0].bitcast(I32))
         for r in range(4):
             nc.sync.dma_start(out=w2_sc[r:P:32, :].bitcast(I32), in_=w2_scales[0, r:16:4, :].bitcast(I32))
 
         ident = keep.tile([P, P], F32, name="ident")
         make_identity(nc, ident[:])
-        bias = keep.tile([P, M], F32, name="bias")
-        bias_v = bias[:].rearrange("p (n u c) -> p u n c", u=2, c=4)
+        bias_banks = []
         for u in range(2):
             bank = y_psum.tile([P, 512], F32, name="y_bank")
             for c in range(4):
                 column = b_col[:, 4 * u + c : 4 * u + c + 1].to_broadcast([P, P])
                 nc.tensor.transpose(bank[:, 128 * c : 128 * c + 128], column, ident[:])
-            nc.scalar.activation(bias_v[:, u], bank[:].rearrange("p (c n) -> p n c", c=4), COPY)
+            bias_banks.append(bank)
 
         w1_bf = keep.tile([P, 4 * H], BF16, name="w1_bf", align_bytes=64)
         w1_dst = w1_bf[:].rearrange("p (t m j) -> p m t j", t=4, j=4)
-        w1_src = w1_raw[:].rearrange("p j (m t) -> p m t j", t=4)
-        nc.vector.tensor_copy(out=w1_dst[:, :W1_VECTOR], in_=w1_src[:, :W1_VECTOR])
-        nc.scalar.activation(w1_dst[:, W1_VECTOR:], w1_src[:, W1_VECTOR:], COPY)
-        x_scales = keep.tile([P, S], U8, name="x_scales", align_bytes=64)
-        nc.vector.tensor_copy(x_scales[:], tab_scales[:].indirect(offsets[:]))
+        nc.scalar.activation(w1_dst[:, :64], w1_low[:].rearrange("p j (m t) -> p m t j", t=4), COPY)
+        nc.vector.tensor_copy(out=w1_dst[:, 64:], in_=w1_high[:].rearrange("p j (m t) -> p m t j", t=4))
         w1_codes = keep.tile([P, H], U32, name="w1_codes", align_bytes=64)
         w1_sc = keep.tile([P, H], U8, name="w1_sc", align_bytes=64)
         nc.vector.quantize_mx(out=w1_codes[:].bitcast(FP8X4), scales=w1_sc[:], in_=w1_bf[:])
+
+        bias = keep.tile([P, M], F32, name="bias", tag="w1_low", align_bytes=64)
+        bias_v = bias[:].rearrange("p (n u c) -> p u n c", u=2, c=4)
+        for u in range(2):
+            nc.scalar.activation(bias_v[:, u], bias_banks[u][:].rearrange("p (c n) -> p n c", c=4), COPY)
 
         x_words = []
         for g in range(2):
@@ -105,8 +115,8 @@ def tile_list_tabmlp_tm_bias_kernel(tc, tab, w1, w2_words, w2_scales, b, offs, o
             h_rounded.append(h_bf)
 
         def quantise(c):
-            codes = ring.tile([P, 128], U32, name="h_codes", align_bytes=64)
-            scales = ring.tile([P, 128], U8, name="h_scales", align_bytes=64)
+            codes = ring.tile([P, 128], U32, name="h_codes", align_bytes=64, bufs=2)
+            scales = ring.tile([P, 128], U8, name="h_scales", align_bytes=64, bufs=2)
             nc.vector.quantize_mx(out=codes[:].bitcast(FP8X4), scales=scales[:], in_=h_rounded[c][:])
             h_codes.append((codes, scales))
 
@@ -145,9 +155,9 @@ def tile_list_tabmlp_tm_bias_kernel(tc, tab, w1, w2_words, w2_scales, b, offs, o
         second_product(0, 512, 512)
         quantise(2)
         second_product(1, 0, 512)
-        quantise(3)
         second_product(1, 512, 512)
+        quantise(3)
         second_product(2, 0, 512)
         second_product(2, 512, 512)
         second_product(3, 0, 512)
-        second_product(3, 512, 512, pieces=2)
+        second_product(3, 512, 512)

@@ -48,17 +48,17 @@ def tile_list_tabmlp_tm_bias_kernel(tc, tab, w1, w2_words, w2_scales, b, offs, o
         nc.sync.dma_start(out=w1_low[:], in_=w1_rows[:, :, : H // 2])
         nc.sync.dma_start(offsets[:], offs)
         nc.sync.dma_start(out=b_col[:], in_=b.rearrange("(n c) -> n c", c=8))
-        nc.sync.dma_start(out=tab_scales[0:P:8, :].bitcast(I32), in_=scales_dram.bitcast(I32))
+        nc.sync.dma_start(out=tab_scales[0:112:7, :].bitcast(I32), in_=scales_dram.bitcast(I32))
         nc.sync.dma_start(out=w1_high[:], in_=w1_rows[:, :, H // 2 :])
         nc.sync.dma_start(out=tab_words[:].bitcast(I32), in_=words_dram.bitcast(I32))
         nc.vector.tensor_copy(gathered_scales[:], tab_scales[:].indirect(offsets[:]))
         for r in range(4):
             nc.sync.dma_start(
-                out=x_scales[r:P:32, :].bitcast(I32), in_=gathered_scales[8 * r : P : 32, :].bitcast(I32)
+                out=x_scales[r:P:32, :].bitcast(I32), in_=gathered_scales[7 * r : 112 : 28, :].bitcast(I32)
             )
         w2_codes = shared.tile([P, 2 * M], U8, name="w2_codes", align_bytes=64, offset=M)
         w2_sc = shared.tile([P, M], U8, name="w2_sc", align_bytes=64, offset=0)
-        nc.gpsimd.memset(w2_sc[:].bitcast(I32), 0)
+        nc.vector.memset(w2_sc[:].bitcast(I32), 0)
         nc.sync.dma_start(out=w2_codes[:].bitcast(I32), in_=w2_words[0].bitcast(I32))
         for r in range(4):
             nc.sync.dma_start(out=w2_sc[r:P:32, :].bitcast(I32), in_=w2_scales[0, r:16:4, :].bitcast(I32))
@@ -76,7 +76,9 @@ def tile_list_tabmlp_tm_bias_kernel(tc, tab, w1, w2_words, w2_scales, b, offs, o
         w1_bf = keep.tile([P, 4 * H], BF16, name="w1_bf", align_bytes=64)
         w1_dst = w1_bf[:].rearrange("p (t m j) -> p m t j", t=4, j=4)
         nc.scalar.activation(w1_dst[:, :64], w1_low[:].rearrange("p j (m t) -> p m t j", t=4), COPY)
-        nc.vector.tensor_copy(out=w1_dst[:, 64:], in_=w1_high[:].rearrange("p j (m t) -> p m t j", t=4))
+        high_src = w1_high[:].rearrange("p j (m t) -> p m t j", t=4)
+        nc.scalar.activation(w1_dst[:, 64 : 64 + 16], high_src[:, :16], COPY)
+        nc.vector.tensor_copy(out=w1_dst[:, 64 + 16 :], in_=high_src[:, 16:])
         w1_codes = keep.tile([P, H], U32, name="w1_codes", align_bytes=64)
         w1_sc = keep.tile([P, H], U8, name="w1_sc", align_bytes=64)
         nc.vector.quantize_mx(out=w1_codes[:].bitcast(FP8X4), scales=w1_sc[:], in_=w1_bf[:])

@@ -7,6 +7,8 @@ K, H, M, T, S = 512, 512, 1024, 2048, 512
 FLOPS = 2 * K * H * S + 2 * H * M * S
 
 P = 128
+BANK = 512
+CHUNK = 128
 F32 = mybir.dt.float32
 BF16 = mybir.dt.bfloat16
 I32 = mybir.dt.int32
@@ -18,6 +20,9 @@ FP4X4 = mybir.dt.float4_e2m1fn_x4
 COPY = mybir.ActivationFunctionType.Copy
 RELU = mybir.ActivationFunctionType.Relu
 ADD = mybir.AluOpType.add
+
+SCALAR_GROUPS = 16
+ROW_STEP = 7
 
 
 def tile_list_tabmlp_tm_bias_kernel(tc, tab, w1, w2_words, w2_scales, b, offs, out):
@@ -48,37 +53,40 @@ def tile_list_tabmlp_tm_bias_kernel(tc, tab, w1, w2_words, w2_scales, b, offs, o
         nc.sync.dma_start(out=w1_low[:], in_=w1_rows[:, :, : H // 2])
         nc.sync.dma_start(offsets[:], offs)
         nc.sync.dma_start(out=b_col[:], in_=b.rearrange("(n c) -> n c", c=8))
-        nc.sync.dma_start(out=tab_scales[0:112:7, :].bitcast(I32), in_=scales_dram.bitcast(I32))
+        nc.sync.dma_start(out=tab_scales[0 : 16 * ROW_STEP : ROW_STEP, :].bitcast(I32), in_=scales_dram.bitcast(I32))
         nc.sync.dma_start(out=w1_high[:], in_=w1_rows[:, :, H // 2 :])
         nc.sync.dma_start(out=tab_words[:].bitcast(I32), in_=words_dram.bitcast(I32))
+
         nc.vector.tensor_copy(gathered_scales[:], tab_scales[:].indirect(offsets[:]))
-        for r in range(4):
+        for row in range(4):
             nc.sync.dma_start(
-                out=x_scales[r:P:32, :].bitcast(I32), in_=gathered_scales[7 * r : 112 : 28, :].bitcast(I32)
+                out=x_scales[row:P:32, :].bitcast(I32),
+                in_=gathered_scales[ROW_STEP * row : 16 * ROW_STEP : 4 * ROW_STEP, :].bitcast(I32),
             )
+
         w2_codes = shared.tile([P, 2 * M], U8, name="w2_codes", align_bytes=64, offset=M)
         w2_sc = shared.tile([P, M], U8, name="w2_sc", align_bytes=64, offset=0)
         nc.vector.memset(w2_sc[:].bitcast(I32), 0)
         nc.sync.dma_start(out=w2_codes[:].bitcast(I32), in_=w2_words[0].bitcast(I32))
-        for r in range(4):
-            nc.sync.dma_start(out=w2_sc[r:P:32, :].bitcast(I32), in_=w2_scales[0, r:16:4, :].bitcast(I32))
+        for row in range(4):
+            nc.sync.dma_start(out=w2_sc[row:P:32, :].bitcast(I32), in_=w2_scales[0, row:16:4, :].bitcast(I32))
 
         ident = keep.tile([P, P], F32, name="ident")
         make_identity(nc, ident[:])
         bias_banks = []
         for u in range(2):
-            bank = y_psum.tile([P, 512], F32, name="y_bank")
+            bank = y_psum.tile([P, BANK], F32, name="y_bank")
             for c in range(4):
                 column = b_col[:, 4 * u + c : 4 * u + c + 1].to_broadcast([P, P])
-                nc.tensor.transpose(bank[:, 128 * c : 128 * c + 128], column, ident[:])
+                nc.tensor.transpose(bank[:, P * c : P * c + P], column, ident[:])
             bias_banks.append(bank)
 
         w1_bf = keep.tile([P, 4 * H], BF16, name="w1_bf", align_bytes=64)
         w1_dst = w1_bf[:].rearrange("p (t m j) -> p m t j", t=4, j=4)
         nc.scalar.activation(w1_dst[:, :64], w1_low[:].rearrange("p j (m t) -> p m t j", t=4), COPY)
         high_src = w1_high[:].rearrange("p j (m t) -> p m t j", t=4)
-        nc.scalar.activation(w1_dst[:, 64 : 64 + 16], high_src[:, :16], COPY)
-        nc.vector.tensor_copy(out=w1_dst[:, 64 + 16 :], in_=high_src[:, 16:])
+        nc.scalar.activation(w1_dst[:, 64 : 64 + SCALAR_GROUPS], high_src[:, :SCALAR_GROUPS], COPY)
+        nc.vector.tensor_copy(out=w1_dst[:, 64 + SCALAR_GROUPS :], in_=high_src[:, SCALAR_GROUPS:])
         w1_codes = keep.tile([P, H], U32, name="w1_codes", align_bytes=64)
         w1_sc = keep.tile([P, H], U8, name="w1_sc", align_bytes=64)
         nc.vector.quantize_mx(out=w1_codes[:].bitcast(FP8X4), scales=w1_sc[:], in_=w1_bf[:])
@@ -90,76 +98,69 @@ def tile_list_tabmlp_tm_bias_kernel(tc, tab, w1, w2_words, w2_scales, b, offs, o
 
         x_words = []
         for g in range(2):
-            words = keep.tile([P, 256], U32, name=f"x_words{g}", align_bytes=64)
+            words = keep.tile([P, S // 2], U32, name=f"x_words{g}", align_bytes=64)
             nc.vector.tensor_copy(words[:], tab_words[:].indirect(offsets[:, 16 * g : 16 * g + 16]))
             x_words.append(words)
 
         h_rounded, h_codes = [], []
 
-        def first_product(c, tag):
-            bank = h_psum.tile([P, 512], F32, name=tag)
-            cols = slice(128 * (c % 2), 128 * (c % 2) + 128)
+        def first_product(chunk, bank_name):
+            bank = h_psum.tile([P, BANK], F32, name=bank_name)
+            cols = slice(CHUNK * (chunk % 2), CHUNK * (chunk % 2) + CHUNK)
             for t in range(4):
-                r = slice(128 * t, 128 * t + 128)
+                quarter = slice(P * t, P * t + P)
                 nc.tensor.matmul_mx(
-                    out=bank[:, r],
-                    lhsT=w1_codes[:, r].bitcast(FP8X4),
-                    lhsT_scale=w1_sc[:, r],
-                    rhs=x_words[c // 2][:, cols].bitcast(FP8X4),
-                    rhs_scale=x_scales[:, 128 * c : 128 * c + 128],
+                    out=bank[:, quarter],
+                    lhsT=w1_codes[:, quarter].bitcast(FP8X4),
+                    lhsT_scale=w1_sc[:, quarter],
+                    rhs=x_words[chunk // 2][:, cols].bitcast(FP8X4),
+                    rhs_scale=x_scales[:, CHUNK * chunk : CHUNK * chunk + CHUNK],
                     start=True,
                     stop=True,
                 )
-            h_bf = ring.tile([P, 512], BF16, name="h_bf", align_bytes=64)
+            h_bf = ring.tile([P, 4 * CHUNK], BF16, name="h_bf", align_bytes=64)
             nc.scalar.activation(
                 h_bf[:].rearrange("p (n t) -> p n t", t=4), bank[:].rearrange("p (t n) -> p n t", t=4), RELU
             )
             h_rounded.append(h_bf)
 
-        def quantise(c):
-            codes = ring.tile([P, 128], U32, name="h_codes", align_bytes=64, bufs=2)
-            scales = ring.tile([P, 128], U8, name="h_scales", align_bytes=64, bufs=2)
-            nc.vector.quantize_mx(out=codes[:].bitcast(FP8X4), scales=scales[:], in_=h_rounded[c][:])
+        def quantise(chunk):
+            codes = ring.tile([P, CHUNK], U32, name="h_codes", align_bytes=64, bufs=2)
+            scales = ring.tile([P, CHUNK], U8, name="h_scales", align_bytes=64, bufs=2)
+            nc.vector.quantize_mx(out=codes[:].bitcast(FP8X4), scales=scales[:], in_=h_rounded[chunk][:])
             h_codes.append((codes, scales))
 
-        def product(c, n0, width, tag):
-            codes, scales = h_codes[c]
-            pool = y_psum if tag == "y_bank" else h_psum
-            bank = pool.tile([P, 512], F32, name=tag)
+        def second_product(chunk, n0, width, bank):
+            codes, scales = h_codes[chunk]
+            cols = slice(n0, n0 + width)
             nc.tensor.matmul_mx(
                 out=bank[:, :width],
                 lhsT=codes[:].bitcast(FP8X4),
                 lhsT_scale=scales[:],
                 rhs=w2_codes[:, 2 * n0 : 2 * (n0 + width)].bitcast(FP4X4),
-                rhs_scale=w2_sc[:, n0 : n0 + width],
+                rhs_scale=w2_sc[:, cols],
                 start=True,
                 stop=True,
             )
-            return bank
+            result = outs.tile([P, BANK], F32, name="result")
+            nc.vector.tensor_tensor(result[:, :width], bank[:, :width], bias[:, cols], ADD)
+            nc.sync.dma_start(out=out[CHUNK * chunk : CHUNK * chunk + CHUNK, cols], in_=result[:, :width])
 
-        def second_product(c, n0, width, pieces=1, tag="y_bank"):
-            bank = product(c, n0, width, tag)
-            step = width // pieces
-            for i in range(pieces):
-                cols = slice(n0 + i * step, n0 + (i + 1) * step)
-                result = outs.tile([P, 512], F32, name="result")
-                nc.vector.tensor_tensor(result[:, :step], bank[:, i * step : (i + 1) * step], bias[:, cols], ADD)
-                nc.sync.dma_start(out=out[128 * c : 128 * c + 128, cols], in_=result[:, :step])
+        def y_bank():
+            return y_psum.tile([P, BANK], F32, name="y_bank")
 
-        first_product(0, "h0")
-        first_product(1, "h1")
-        first_product(2, "h2")
+        for chunk in range(3):
+            first_product(chunk, f"h{chunk}")
         quantise(0)
-        second_product(0, 0, 256, tag="h3")
-        second_product(0, 256, 256)
-        first_product(3, "h3")
+        second_product(0, 0, BANK // 2, y_bank())
+        second_product(0, BANK // 2, BANK // 2, h_psum.tile([P, BANK], F32, name="h3"))
         quantise(1)
-        second_product(0, 512, 512)
+        second_product(0, BANK, BANK, y_bank())
         quantise(2)
-        second_product(1, 0, 512)
-        second_product(1, 512, 512)
+        second_product(1, 0, BANK, y_bank())
+        first_product(3, "h3")
+        second_product(1, BANK, BANK, y_bank())
         quantise(3)
-        second_product(2, 0, 512)
-        second_product(2, 512, 512)
-        second_product(3, 0, 512)
-        second_product(3, 512, 512)
+        for chunk in (2, 3):
+            for n0 in (0, BANK):
+                second_product(chunk, n0, BANK, y_bank())

@@ -21,7 +21,7 @@ COPY = mybir.ActivationFunctionType.Copy
 RELU = mybir.ActivationFunctionType.Relu
 ADD = mybir.AluOpType.add
 
-SCALAR_GROUPS = 16
+SCALAR_GROUPS = 64
 ROW_STEP = 7
 
 
@@ -39,8 +39,7 @@ def tile_list_tabmlp_tm_bias_kernel(tc, tab, w1, w2_words, w2_scales, b, offs, o
         b_col = keep.tile([P, 8], F32, name="b_col")
         tab_words = keep.tile([P, T], U32, name="tab_words", align_bytes=64)
         tab_scales = shared.tile([P, T], U8, name="tab_scales", align_bytes=64, offset=0)
-        w1_low = keep.tile([P, 4, H // 2], F32, name="w1_low", tag="w1_low", align_bytes=64)
-        w1_high = keep.tile([P, 4, H // 2], F32, name="w1_high", align_bytes=64)
+        w1_raw = keep.tile([P, 4, H], F32, name="w1_raw", tag="w1_raw", align_bytes=64)
         scales_dram = tab[0, 512 * T : 528 * T].rearrange("(q t) -> q t", q=16)
         words_dram = tab[0, 0 : 512 * T].rearrange("(p b) -> p b", p=P)
 
@@ -50,11 +49,11 @@ def tile_list_tabmlp_tm_bias_kernel(tc, tab, w1, w2_words, w2_scales, b, offs, o
         nc.vector.memset(x_scales[:].bitcast(I32), 0)
 
         w1_rows = w1.rearrange("(p j) r -> p j r", j=4)
-        nc.sync.dma_start(out=w1_low[:], in_=w1_rows[:, :, : H // 2])
+        nc.sync.dma_start(out=w1_raw[:, :1], in_=w1_rows[:, :1])
         nc.sync.dma_start(offsets[:], offs)
         nc.sync.dma_start(out=b_col[:], in_=b.rearrange("(n c) -> n c", c=8))
         nc.sync.dma_start(out=tab_scales[0 : 16 * ROW_STEP : ROW_STEP, :].bitcast(I32), in_=scales_dram.bitcast(I32))
-        nc.sync.dma_start(out=w1_high[:], in_=w1_rows[:, :, H // 2 :])
+        nc.sync.dma_start(out=w1_raw[:, 1:], in_=w1_rows[:, 1:])
         nc.sync.dma_start(out=tab_words[:].bitcast(I32), in_=words_dram.bitcast(I32))
 
         nc.vector.tensor_copy(gathered_scales[:], tab_scales[:].indirect(offsets[:]))
@@ -83,15 +82,15 @@ def tile_list_tabmlp_tm_bias_kernel(tc, tab, w1, w2_words, w2_scales, b, offs, o
 
         w1_bf = keep.tile([P, 4 * H], BF16, name="w1_bf", align_bytes=64)
         w1_dst = w1_bf[:].rearrange("p (t m j) -> p m t j", t=4, j=4)
-        nc.scalar.activation(w1_dst[:, :64], w1_low[:].rearrange("p j (m t) -> p m t j", t=4), COPY)
-        high_src = w1_high[:].rearrange("p j (m t) -> p m t j", t=4)
-        nc.scalar.activation(w1_dst[:, 64 : 64 + SCALAR_GROUPS], high_src[:, :SCALAR_GROUPS], COPY)
-        nc.vector.tensor_copy(out=w1_dst[:, 64 + SCALAR_GROUPS :], in_=high_src[:, SCALAR_GROUPS:])
+        w1_src = w1_raw[:].rearrange("p j (m t) -> p m t j", t=4)
+        for pair in (slice(0, 1), slice(1, 4)):
+            nc.scalar.activation(w1_dst[:, :SCALAR_GROUPS, :, pair], w1_src[:, :SCALAR_GROUPS, :, pair], COPY)
+        nc.vector.tensor_copy(out=w1_dst[:, SCALAR_GROUPS:], in_=w1_src[:, SCALAR_GROUPS:])
         w1_codes = keep.tile([P, H], U32, name="w1_codes", align_bytes=64)
         w1_sc = keep.tile([P, H], U8, name="w1_sc", align_bytes=64)
         nc.vector.quantize_mx(out=w1_codes[:].bitcast(FP8X4), scales=w1_sc[:], in_=w1_bf[:])
 
-        bias = keep.tile([P, M], F32, name="bias", tag="w1_low", align_bytes=64)
+        bias = keep.tile([P, M], F32, name="bias", tag="w1_raw", align_bytes=64)
         bias_v = bias[:].rearrange("p (n u c) -> p u n c", u=2, c=4)
         for u in range(2):
             nc.scalar.activation(bias_v[:, u], bias_banks[u][:].rearrange("p (c n) -> p n c", c=4), COPY)

@@ -103,6 +103,11 @@ def tile_list_tabmlp_tm_bias_kernel(tc, tab, w1, w2_words, w2_scales, b, offs, o
 
         h_rounded, h_codes = [], []
 
+        def parts(chunk):
+            if chunk == 0:
+                return [slice(0, CHUNK // 2), slice(CHUNK // 2, CHUNK)]
+            return [slice(0, CHUNK)]
+
         def first_product(chunk, bank_name):
             bank = h_psum.tile([P, BANK], F32, name=bank_name)
             cols = slice(CHUNK * (chunk % 2), CHUNK * (chunk % 2) + CHUNK)
@@ -118,15 +123,21 @@ def tile_list_tabmlp_tm_bias_kernel(tc, tab, w1, w2_words, w2_scales, b, offs, o
                     stop=True,
                 )
             h_bf = ring.tile([P, 4 * CHUNK], BF16, name="h_bf", align_bytes=64)
-            nc.scalar.activation(
-                h_bf[:].rearrange("p (n t) -> p n t", t=4), bank[:].rearrange("p (t n) -> p n t", t=4), RELU
-            )
+            dst = h_bf[:].rearrange("p (n t) -> p n t", t=4)
+            src = bank[:].rearrange("p (t n) -> p n t", t=4)
+            for part in parts(chunk):
+                nc.scalar.activation(dst[:, part], src[:, part], RELU)
             h_rounded.append(h_bf)
 
         def quantise(chunk):
             codes = ring.tile([P, CHUNK], U32, name="h_codes", align_bytes=64, bufs=2)
             scales = ring.tile([P, CHUNK], U8, name="h_scales", align_bytes=64, bufs=2)
-            nc.vector.quantize_mx(out=codes[:].bitcast(FP8X4), scales=scales[:], in_=h_rounded[chunk][:])
+            for part in parts(chunk):
+                nc.vector.quantize_mx(
+                    out=codes[:, part].bitcast(FP8X4),
+                    scales=scales[:, part],
+                    in_=h_rounded[chunk][:, 4 * part.start : 4 * part.stop],
+                )
             h_codes.append((codes, scales))
 
         def second_product(chunk, n0, width, bank):

@@ -95,6 +95,16 @@ def tile_list_tabmlp_tm_bias_kernel(tc, tab, w1, w2_words, w2_scales, b, offs, o
         for u in range(2):
             nc.scalar.activation(bias_v[:, u], bias_banks[u][:].rearrange("p (c n) -> p n c", c=4), COPY)
 
+        nc.tensor.matmul_mx(
+            out=h_psum.tile([P, BANK], F32, name="h3")[:],
+            lhsT=w1_codes[:, :P].bitcast(FP8X4),
+            lhsT_scale=w1_sc[:, :P],
+            rhs=tab_words[:, :BANK].bitcast(FP8X4),
+            rhs_scale=w1_sc[:],
+            start=True,
+            stop=True,
+        )
+
         x_words = []
         for g in range(2):
             words = keep.tile([P, S // 2], U32, name=f"x_words{g}", align_bytes=64)
@@ -140,21 +150,33 @@ def tile_list_tabmlp_tm_bias_kernel(tc, tab, w1, w2_words, w2_scales, b, offs, o
                 )
             h_codes.append((codes, scales))
 
-        def second_product(chunk, n0, width, bank):
+        def second_pass(chunk, n0, width, bank):
             codes, scales = h_codes[chunk]
-            cols = slice(n0, n0 + width)
             nc.tensor.matmul_mx(
                 out=bank[:, :width],
                 lhsT=codes[:].bitcast(FP8X4),
                 lhsT_scale=scales[:],
                 rhs=w2_codes[:, 2 * n0 : 2 * (n0 + width)].bitcast(FP4X4),
-                rhs_scale=w2_sc[:, cols],
+                rhs_scale=w2_sc[:, n0 : n0 + width],
                 start=True,
                 stop=True,
             )
-            result = outs.tile([P, BANK], F32, name="result")
-            nc.vector.tensor_tensor(result[:, :width], bank[:, :width], bias[:, cols], ADD)
-            nc.sync.dma_start(out=out[CHUNK * chunk : CHUNK * chunk + CHUNK, cols], in_=result[:, :width])
+            return bank[:, :width]
+
+        def add_bias(result, y, n0):
+            nc.vector.tensor_tensor(result, y, bias[:, n0 : n0 + y.shape[1]], ADD)
+
+        def store(chunk, n0, result):
+            rows = slice(CHUNK * chunk, CHUNK * chunk + CHUNK)
+            nc.sync.dma_start(out=out[rows, n0 : n0 + result.shape[1]], in_=result)
+
+        def new_result():
+            return outs.tile([P, BANK], F32, name="result")
+
+        def second_product(chunk, n0, width, bank):
+            result = new_result()
+            add_bias(result[:, :width], second_pass(chunk, n0, width, bank), n0)
+            store(chunk, n0, result[:, :width])
 
         def y_bank():
             return y_psum.tile([P, BANK], F32, name="y_bank")

@@ -9,6 +9,7 @@ FLOPS = 2 * K * H * S + 2 * H * M * S
 P = 128
 BANK = 512
 CHUNK = 128
+CHUNKS = S // CHUNK
 F32 = mybir.dt.float32
 BF16 = mybir.dt.bfloat16
 I32 = mybir.dt.int32
@@ -30,10 +31,12 @@ def tile_list_tabmlp_tm_bias_kernel(tc, tab, w1, w2_words, w2_scales, b, offs, o
     with ExitStack() as ctx:
         keep = ctx.enter_context(tc.tile_pool(name="keep", bufs=1))
         shared = ctx.enter_context(tc.tile_pool(name="shared", bufs=1))
-        ring = ctx.enter_context(tc.tile_pool(name="ring", bufs=4))
+        ring = ctx.enter_context(tc.tile_pool(name="ring", bufs=CHUNKS))
         outs = ctx.enter_context(tc.tile_pool(name="outs", bufs=10))
-        h_psum = ctx.enter_context(tc.psum_pool(name="h_psum", bufs=1))
-        y_psum = ctx.enter_context(tc.psum_pool(name="y_psum", bufs=4))
+        psum = ctx.enter_context(tc.psum_pool(name="psum", bufs=1))
+
+        def bank(number):
+            return psum.tile([P, BANK], F32, name=f"bank{number}")
 
         offsets = keep.tile([P, S // 16], U16, name="offsets")
         b_col = keep.tile([P, 8], F32, name="b_col")
@@ -72,19 +75,17 @@ def tile_list_tabmlp_tm_bias_kernel(tc, tab, w1, w2_words, w2_scales, b, offs, o
 
         ident = keep.tile([P, P], F32, name="ident")
         make_identity(nc, ident[:])
-        bias_banks = []
+        bias_banks = [bank(0), bank(1)]
         for u in range(2):
-            bank = y_psum.tile([P, BANK], F32, name="y_bank")
             for c in range(4):
                 column = b_col[:, 4 * u + c : 4 * u + c + 1].to_broadcast([P, P])
-                nc.tensor.transpose(bank[:, P * c : P * c + P], column, ident[:])
-            bias_banks.append(bank)
+                nc.tensor.transpose(bias_banks[u][:, P * c : P * c + P], column, ident[:])
 
         w1_bf = keep.tile([P, 4 * H], BF16, name="w1_bf", align_bytes=64)
         w1_dst = w1_bf[:].rearrange("p (t m j) -> p m t j", t=4, j=4)
         w1_src = w1_raw[:].rearrange("p j (m t) -> p m t j", t=4)
-        for pair in (slice(0, 1), slice(1, 4)):
-            nc.scalar.activation(w1_dst[:, :SCALAR_GROUPS, :, pair], w1_src[:, :SCALAR_GROUPS, :, pair], COPY)
+        for rows in (slice(0, 1), slice(1, 4)):
+            nc.scalar.activation(w1_dst[:, :SCALAR_GROUPS, :, rows], w1_src[:, :SCALAR_GROUPS, :, rows], COPY)
         nc.vector.tensor_copy(out=w1_dst[:, SCALAR_GROUPS:], in_=w1_src[:, SCALAR_GROUPS:])
         w1_codes = keep.tile([P, H], U32, name="w1_codes", align_bytes=64)
         w1_sc = keep.tile([P, H], U8, name="w1_sc", align_bytes=64)
@@ -96,20 +97,14 @@ def tile_list_tabmlp_tm_bias_kernel(tc, tab, w1, w2_words, w2_scales, b, offs, o
             nc.scalar.activation(bias_v[:, u], bias_banks[u][:].rearrange("p (c n) -> p n c", c=4), COPY)
 
         nc.tensor.matmul_mx(
-            out=h_psum.tile([P, BANK], F32, name="h3")[:],
+            out=bank(0)[:],
             lhsT=w1_codes[:, :P].bitcast(FP8X4),
             lhsT_scale=w1_sc[:, :P],
-            rhs=tab_words[:, :BANK].bitcast(FP8X4),
+            rhs=w1_codes[:].bitcast(FP8X4),
             rhs_scale=w1_sc[:],
             start=True,
             stop=True,
         )
-
-        x_words = []
-        for g in range(2):
-            words = keep.tile([P, S // 2], U32, name=f"x_words{g}", align_bytes=64)
-            nc.vector.tensor_copy(words[:], tab_words[:].indirect(offsets[:, 16 * g : 16 * g + 16]))
-            x_words.append(words)
 
         h_rounded, h_codes = [], []
 
@@ -118,23 +113,27 @@ def tile_list_tabmlp_tm_bias_kernel(tc, tab, w1, w2_words, w2_scales, b, offs, o
                 return [slice(0, CHUNK // 2), slice(CHUNK // 2, CHUNK)]
             return [slice(0, CHUNK)]
 
-        def first_product(chunk, bank_name):
-            bank = h_psum.tile([P, BANK], F32, name=bank_name)
-            cols = slice(CHUNK * (chunk % 2), CHUNK * (chunk % 2) + CHUNK)
+        def look_up(chunk):
+            words = ring.tile([P, CHUNK], U32, name="x_words", align_bytes=64)
+            columns = slice(CHUNK // 16 * chunk, CHUNK // 16 * (chunk + 1))
+            nc.vector.tensor_copy(words[:], tab_words[:].indirect(offsets[:, columns]))
+            return words
+
+        def first_product(chunk, h_bank):
             for t in range(4):
                 quarter = slice(P * t, P * t + P)
                 nc.tensor.matmul_mx(
-                    out=bank[:, quarter],
+                    out=h_bank[:, quarter],
                     lhsT=w1_codes[:, quarter].bitcast(FP8X4),
                     lhsT_scale=w1_sc[:, quarter],
-                    rhs=x_words[chunk // 2][:, cols].bitcast(FP8X4),
+                    rhs=x_words[chunk][:].bitcast(FP8X4),
                     rhs_scale=x_scales[:, CHUNK * chunk : CHUNK * chunk + CHUNK],
                     start=True,
                     stop=True,
                 )
             h_bf = ring.tile([P, 4 * CHUNK], BF16, name="h_bf", align_bytes=64)
             dst = h_bf[:].rearrange("p (n t) -> p n t", t=4)
-            src = bank[:].rearrange("p (t n) -> p n t", t=4)
+            src = h_bank[:].rearrange("p (t n) -> p n t", t=4)
             for part in parts(chunk):
                 nc.scalar.activation(dst[:, part], src[:, part], RELU)
             h_rounded.append(h_bf)
@@ -150,10 +149,10 @@ def tile_list_tabmlp_tm_bias_kernel(tc, tab, w1, w2_words, w2_scales, b, offs, o
                 )
             h_codes.append((codes, scales))
 
-        def second_pass(chunk, n0, width, bank):
+        def second_product(chunk, n0, width, y_bank):
             codes, scales = h_codes[chunk]
             nc.tensor.matmul_mx(
-                out=bank[:, :width],
+                out=y_bank[:, :width],
                 lhsT=codes[:].bitcast(FP8X4),
                 lhsT_scale=scales[:],
                 rhs=w2_codes[:, 2 * n0 : 2 * (n0 + width)].bitcast(FP4X4),
@@ -161,38 +160,25 @@ def tile_list_tabmlp_tm_bias_kernel(tc, tab, w1, w2_words, w2_scales, b, offs, o
                 start=True,
                 stop=True,
             )
-            return bank[:, :width]
+            result = outs.tile([P, BANK], F32, name="result")
+            nc.vector.tensor_tensor(result[:, :width], y_bank[:, :width], bias[:, n0 : n0 + width], ADD)
+            nc.sync.dma_start(out=out[CHUNK * chunk : CHUNK * chunk + CHUNK, n0 : n0 + width], in_=result[:, :width])
 
-        def add_bias(result, y, n0):
-            nc.vector.tensor_tensor(result, y, bias[:, n0 : n0 + y.shape[1]], ADD)
-
-        def store(chunk, n0, result):
-            rows = slice(CHUNK * chunk, CHUNK * chunk + CHUNK)
-            nc.sync.dma_start(out=out[rows, n0 : n0 + result.shape[1]], in_=result)
-
-        def new_result():
-            return outs.tile([P, BANK], F32, name="result")
-
-        def second_product(chunk, n0, width, bank):
-            result = new_result()
-            add_bias(result[:, :width], second_pass(chunk, n0, width, bank), n0)
-            store(chunk, n0, result[:, :width])
-
-        def y_bank():
-            return y_psum.tile([P, BANK], F32, name="y_bank")
+        x_words = [look_up(chunk) for chunk in range(CHUNKS)]
 
         for chunk in range(3):
-            first_product(chunk, f"h{chunk}")
+            first_product(chunk, bank(2 + chunk))
         quantise(0)
-        second_product(0, 0, BANK // 2, y_bank())
-        second_product(0, BANK // 2, BANK // 2, h_psum.tile([P, BANK], F32, name="h3"))
+        second_product(0, 0, BANK // 2, bank(6))
+        second_product(0, BANK // 2, BANK // 2, bank(5))
         quantise(1)
-        second_product(0, BANK, BANK, y_bank())
+        second_product(0, BANK, BANK, bank(7))
         quantise(2)
-        second_product(1, 0, BANK, y_bank())
-        first_product(3, "h3")
-        second_product(1, BANK, BANK, y_bank())
+        second_product(1, 0, BANK, bank(0))
+        first_product(3, bank(5))
+        second_product(1, BANK, BANK, bank(1))
         quantise(3)
-        for chunk in (2, 3):
-            for n0 in (0, BANK):
-                second_product(chunk, n0, BANK, y_bank())
+        second_product(2, 0, BANK, bank(6))
+        second_product(2, BANK, BANK, bank(7))
+        second_product(3, 0, BANK, bank(0))
+        second_product(3, BANK, BANK, bank(1))

@@ -149,19 +149,23 @@ def tile_list_tabmlp_tm_bias_kernel(tc, tab, w1, w2_words, w2_scales, b, offs, o
                 )
             h_codes.append((codes, scales))
 
-        def second_product(chunk, n0, width, y_bank):
+        def second_product(chunk, n0, width, *y_banks):
             codes, scales = h_codes[chunk]
-            nc.tensor.matmul_mx(
-                out=y_bank[:, :width],
-                lhsT=codes[:].bitcast(FP8X4),
-                lhsT_scale=scales[:],
-                rhs=w2_codes[:, 2 * n0 : 2 * (n0 + width)].bitcast(FP4X4),
-                rhs_scale=w2_sc[:, n0 : n0 + width],
-                start=True,
-                stop=True,
-            )
             result = outs.tile([P, BANK], F32, name="result")
-            nc.vector.tensor_tensor(result[:, :width], y_bank[:, :width], bias[:, n0 : n0 + width], ADD)
+            share = width // len(y_banks)
+            for i, y_bank in enumerate(y_banks):
+                first = n0 + share * i
+                nc.tensor.matmul_mx(
+                    out=y_bank[:, :share],
+                    lhsT=codes[:].bitcast(FP8X4),
+                    lhsT_scale=scales[:],
+                    rhs=w2_codes[:, 2 * first : 2 * (first + share)].bitcast(FP4X4),
+                    rhs_scale=w2_sc[:, first : first + share],
+                    start=True,
+                    stop=True,
+                )
+                piece = result[:, share * i : share * (i + 1)]
+                nc.vector.tensor_tensor(piece, y_bank[:, :share], bias[:, first : first + share], ADD)
             nc.sync.dma_start(out=out[CHUNK * chunk : CHUNK * chunk + CHUNK, n0 : n0 + width], in_=result[:, :width])
 
         x_words = [look_up(chunk) for chunk in range(CHUNKS)]
@@ -169,16 +173,16 @@ def tile_list_tabmlp_tm_bias_kernel(tc, tab, w1, w2_words, w2_scales, b, offs, o
         for chunk in range(3):
             first_product(chunk, bank(2 + chunk))
         quantise(0)
-        second_product(0, 0, BANK // 2, bank(6))
-        second_product(0, BANK // 2, BANK // 2, bank(5))
         quantise(1)
-        second_product(0, BANK, BANK, bank(7))
-        quantise(2)
-        second_product(1, 0, BANK, bank(0))
+        second_product(0, 0, BANK // 2, bank(5))
+        second_product(0, BANK // 2, BANK // 2, bank(6))
+        second_product(0, BANK, BANK, bank(7), bank(0))
         first_product(3, bank(5))
-        second_product(1, BANK, BANK, bank(1))
+        quantise(2)
+        second_product(1, 0, BANK, bank(1))
+        second_product(1, BANK, BANK, bank(6))
         quantise(3)
-        second_product(2, 0, BANK, bank(6))
-        second_product(2, BANK, BANK, bank(7))
-        second_product(3, 0, BANK, bank(0))
-        second_product(3, BANK, BANK, bank(1))
+        second_product(2, 0, BANK, bank(2))
+        second_product(2, BANK, BANK, bank(3))
+        second_product(3, 0, BANK, bank(4))
+        second_product(3, BANK, BANK, bank(7))

@@ -151,7 +151,7 @@ def tile_list_tabmlp_tm_bias_kernel(tc, tab, w1, w2_words, w2_scales, b, offs, o
 
         def second_product(chunk, n0, width, *y_banks):
             codes, scales = h_codes[chunk]
-            result = outs.tile([P, BANK], F32, name="result")
+            result = outs.tile([P, M], F32, name="result")
             share = width // len(y_banks)
             for i, y_bank in enumerate(y_banks):
                 first = n0 + share * i
@@ -184,5 +184,4 @@ def tile_list_tabmlp_tm_bias_kernel(tc, tab, w1, w2_words, w2_scales, b, offs, o
         quantise(3)
         second_product(2, 0, BANK, bank(2))
         second_product(2, BANK, BANK, bank(3))
-        second_product(3, 0, BANK, bank(4))
-        second_product(3, BANK, BANK, bank(7))
+        second_product(3, 0, M, bank(4), bank(7))

@@ -149,24 +149,30 @@ def tile_list_tabmlp_tm_bias_kernel(tc, tab, w1, w2_words, w2_scales, b, offs, o
                 )
             h_codes.append((codes, scales))
 
-        def second_product(chunk, n0, width, *y_banks):
+        def second_pass(chunk, n0, width, y_bank):
             codes, scales = h_codes[chunk]
-            result = outs.tile([P, M], F32, name="result")
-            share = width // len(y_banks)
-            for i, y_bank in enumerate(y_banks):
-                first = n0 + share * i
-                nc.tensor.matmul_mx(
-                    out=y_bank[:, :share],
-                    lhsT=codes[:].bitcast(FP8X4),
-                    lhsT_scale=scales[:],
-                    rhs=w2_codes[:, 2 * first : 2 * (first + share)].bitcast(FP4X4),
-                    rhs_scale=w2_sc[:, first : first + share],
-                    start=True,
-                    stop=True,
-                )
-                piece = result[:, share * i : share * (i + 1)]
-                nc.vector.tensor_tensor(piece, y_bank[:, :share], bias[:, first : first + share], ADD)
-            nc.sync.dma_start(out=out[CHUNK * chunk : CHUNK * chunk + CHUNK, n0 : n0 + width], in_=result[:, :width])
+            nc.tensor.matmul_mx(
+                out=y_bank[:, :width],
+                lhsT=codes[:].bitcast(FP8X4),
+                lhsT_scale=scales[:],
+                rhs=w2_codes[:, 2 * n0 : 2 * (n0 + width)].bitcast(FP4X4),
+                rhs_scale=w2_sc[:, n0 : n0 + width],
+                start=True,
+                stop=True,
+            )
+            return y_bank[:, :width]
+
+        def block(chunk, n0, width, y_bank, result):
+            nc.vector.tensor_tensor(result, second_pass(chunk, n0, width, y_bank), bias[:, n0 : n0 + width], ADD)
+
+        def blocks(chunk, n0, *pieces):
+            total = sum(width for width, y_bank in pieces)
+            result = outs.tile([P, BANK], F32, name="result")
+            done = 0
+            for width, y_bank in pieces:
+                block(chunk, n0 + done, width, y_bank, result[:, done : done + width])
+                done = done + width
+            nc.sync.dma_start(out=out[CHUNK * chunk : CHUNK * chunk + CHUNK, n0 : n0 + total], in_=result[:, :total])
 
         x_words = [look_up(chunk) for chunk in range(CHUNKS)]
 
@@ -174,14 +180,15 @@ def tile_list_tabmlp_tm_bias_kernel(tc, tab, w1, w2_words, w2_scales, b, offs, o
             first_product(chunk, bank(2 + chunk))
         quantise(0)
         quantise(1)
-        second_product(0, 0, BANK // 2, bank(5))
-        second_product(0, BANK // 2, BANK // 2, bank(6))
-        second_product(0, BANK, BANK, bank(7), bank(0))
+        blocks(0, 0, (128, bank(5)))
+        blocks(0, 128, (128, bank(6)), (256, bank(7)))
+        blocks(0, BANK, (256, bank(0)), (256, bank(1)))
         first_product(3, bank(5))
+        blocks(1, 0, (BANK, bank(6)))
         quantise(2)
-        second_product(1, 0, BANK, bank(1))
-        second_product(1, BANK, BANK, bank(6))
+        blocks(1, BANK, (BANK, bank(7)))
         quantise(3)
-        second_product(2, 0, BANK, bank(2))
-        second_product(2, BANK, BANK, bank(3))
-        second_product(3, 0, M, bank(4), bank(7))
+        blocks(2, 0, (BANK, bank(2)))
+        blocks(2, BANK, (BANK, bank(3)))
+        blocks(3, 0, (BANK, bank(4)))
+        blocks(3, BANK, (BANK, bank(0)))

@@ -23,7 +23,7 @@ RELU = mybir.ActivationFunctionType.Relu
 ADD = mybir.AluOpType.add
 
 SCALAR_GROUPS = 64
-ROW_STEP = 7
+ROW_STEP = 8
 
 
 def tile_list_tabmlp_tm_bias_kernel(tc, tab, w1, w2_words, w2_scales, b, offs, out):
@@ -49,7 +49,6 @@ def tile_list_tabmlp_tm_bias_kernel(tc, tab, w1, w2_words, w2_scales, b, offs, o
         gathered_scales = keep.tile([P, S], U8, name="gathered_scales", align_bytes=64)
         x_scales = keep.tile([P, S], U8, name="x_scales", align_bytes=64)
         nc.vector.memset(tab_scales[:].bitcast(I32), 0)
-        nc.vector.memset(x_scales[:].bitcast(I32), 0)
 
         w1_rows = w1.rearrange("(p j) r -> p j r", j=4)
         nc.sync.dma_start(out=w1_raw[:, :1], in_=w1_rows[:, :1])
@@ -60,7 +59,8 @@ def tile_list_tabmlp_tm_bias_kernel(tc, tab, w1, w2_words, w2_scales, b, offs, o
         nc.sync.dma_start(out=tab_words[:].bitcast(I32), in_=words_dram.bitcast(I32))
 
         nc.vector.tensor_copy(gathered_scales[:], tab_scales[:].indirect(offsets[:]))
-        for row in range(4):
+        nc.vector.tensor_copy(x_scales[:].bitcast(I32), gathered_scales[:].bitcast(I32))
+        for row in range(1, 4):
             nc.sync.dma_start(
                 out=x_scales[row:P:32, :].bitcast(I32),
                 in_=gathered_scales[ROW_STEP * row : 16 * ROW_STEP : 4 * ROW_STEP, :].bitcast(I32),

@@ -23,7 +23,7 @@ RELU = mybir.ActivationFunctionType.Relu
 ADD = mybir.AluOpType.add
 
 SCALAR_GROUPS = 64
-ROW_STEP = 8
+ROW_START, ROW_STEP = 11, 7
 
 
 def tile_list_tabmlp_tm_bias_kernel(tc, tab, w1, w2_words, w2_scales, b, offs, out):
@@ -49,21 +49,22 @@ def tile_list_tabmlp_tm_bias_kernel(tc, tab, w1, w2_words, w2_scales, b, offs, o
         gathered_scales = keep.tile([P, S], U8, name="gathered_scales", align_bytes=64)
         x_scales = keep.tile([P, S], U8, name="x_scales", align_bytes=64)
         nc.vector.memset(tab_scales[:].bitcast(I32), 0)
+        nc.vector.memset(x_scales[:].bitcast(I32), 0)
 
         w1_rows = w1.rearrange("(p j) r -> p j r", j=4)
         nc.sync.dma_start(out=w1_raw[:, :1], in_=w1_rows[:, :1])
         nc.sync.dma_start(offsets[:], offs)
         nc.sync.dma_start(out=b_col[:], in_=b.rearrange("(n c) -> n c", c=8))
-        nc.sync.dma_start(out=tab_scales[0 : 16 * ROW_STEP : ROW_STEP, :].bitcast(I32), in_=scales_dram.bitcast(I32))
+        nc.sync.dma_start(out=tab_scales[ROW_START : ROW_START + 16 * ROW_STEP : ROW_STEP, :].bitcast(I32), in_=scales_dram.bitcast(I32))
         nc.sync.dma_start(out=w1_raw[:, 1:], in_=w1_rows[:, 1:])
         nc.sync.dma_start(out=tab_words[:].bitcast(I32), in_=words_dram.bitcast(I32))
 
         nc.vector.tensor_copy(gathered_scales[:], tab_scales[:].indirect(offsets[:]))
-        nc.vector.tensor_copy(x_scales[:].bitcast(I32), gathered_scales[:].bitcast(I32))
-        for row in range(1, 4):
+        for row in range(4):
+            first = ROW_START + ROW_STEP * row
             nc.sync.dma_start(
                 out=x_scales[row:P:32, :].bitcast(I32),
-                in_=gathered_scales[ROW_STEP * row : 16 * ROW_STEP : 4 * ROW_STEP, :].bitcast(I32),
+                in_=gathered_scales[first : first + 12 * ROW_STEP + 1 : 4 * ROW_STEP, :].bitcast(I32),
             )
 
         w2_codes = shared.tile([P, 2 * M], U8, name="w2_codes", align_bytes=64, offset=M)
@@ -106,10 +107,11 @@ def tile_list_tabmlp_tm_bias_kernel(tc, tab, w1, w2_words, w2_scales, b, offs, o
             stop=True,
         )
 
-        h_rounded, h_codes = [], []
+        h_rounded = [ring.tile([P, 4 * CHUNK], BF16, name="h_bf", align_bytes=64) for chunk in range(CHUNKS)]
+        h_codes = []
 
         def parts(chunk):
-            if chunk == 0:
+            if chunk < 2:
                 return [slice(0, CHUNK // 2), slice(CHUNK // 2, CHUNK)]
             return [slice(0, CHUNK)]
 
@@ -119,11 +121,11 @@ def tile_list_tabmlp_tm_bias_kernel(tc, tab, w1, w2_words, w2_scales, b, offs, o
             nc.vector.tensor_copy(words[:], tab_words[:].indirect(offsets[:, columns]))
             return words
 
-        def first_product(chunk, h_bank):
-            for t in range(4):
+        def first_product(chunk, h_bank, planes=range(4)):
+            for place, t in enumerate(planes):
                 quarter = slice(P * t, P * t + P)
                 nc.tensor.matmul_mx(
-                    out=h_bank[:, quarter],
+                    out=h_bank[:, P * place : P * place + P],
                     lhsT=w1_codes[:, quarter].bitcast(FP8X4),
                     lhsT_scale=w1_sc[:, quarter],
                     rhs=x_words[chunk][:].bitcast(FP8X4),
@@ -131,12 +133,10 @@ def tile_list_tabmlp_tm_bias_kernel(tc, tab, w1, w2_words, w2_scales, b, offs, o
                     start=True,
                     stop=True,
                 )
-            h_bf = ring.tile([P, 4 * CHUNK], BF16, name="h_bf", align_bytes=64)
-            dst = h_bf[:].rearrange("p (n t) -> p n t", t=4)
-            src = h_bank[:].rearrange("p (t n) -> p n t", t=4)
+            dst = h_rounded[chunk][:].rearrange("p (n t) -> p n t", t=4)[:, :, planes.start : planes.stop]
+            src = h_bank[:, : P * len(planes)].rearrange("p (t n) -> p n t", t=len(planes))
             for part in parts(chunk):
                 nc.scalar.activation(dst[:, part], src[:, part], RELU)
-            h_rounded.append(h_bf)
 
         def quantise(chunk):
             codes = ring.tile([P, CHUNK], U32, name="h_codes", align_bytes=64, bufs=2)
@@ -176,19 +176,21 @@ def tile_list_tabmlp_tm_bias_kernel(tc, tab, w1, w2_words, w2_scales, b, offs, o
 
         x_words = [look_up(chunk) for chunk in range(CHUNKS)]
 
-        for chunk in range(3):
-            first_product(chunk, bank(2 + chunk))
+        first_product(0, bank(2))
+        first_product(1, bank(3))
+        first_product(2, bank(4), range(2))
         quantise(0)
         quantise(1)
         blocks(0, 0, (128, bank(5)))
         blocks(0, 128, (128, bank(6)), (256, bank(7)))
         blocks(0, BANK, (256, bank(0)), (256, bank(1)))
-        first_product(3, bank(5))
-        blocks(1, 0, (BANK, bank(6)))
+        first_product(2, bank(5), range(2, 4))
+        blocks(1, 0, (BANK, bank(2)))
+        first_product(3, bank(6))
         quantise(2)
         blocks(1, BANK, (BANK, bank(7)))
         quantise(3)
-        blocks(2, 0, (BANK, bank(2)))
-        blocks(2, BANK, (BANK, bank(3)))
-        blocks(3, 0, (BANK, bank(4)))
-        blocks(3, BANK, (BANK, bank(0)))
+        blocks(2, 0, (256, bank(3)), (256, bank(4)))
+        blocks(2, BANK, (BANK, bank(5)))
+        blocks(3, 0, (BANK, bank(0)))
+        blocks(3, BANK, (BANK, bank(1)))

@@ -1,7 +1,6 @@
 from contextlib import ExitStack
 
 import concourse.mybir as mybir
-from concourse.masks import make_identity
 
 K, H, M, T, S = 512, 512, 1024, 2048, 512
 FLOPS = 2 * K * H * S + 2 * H * M * S
@@ -10,6 +9,7 @@ P = 128
 BANK = 512
 CHUNK = 128
 CHUNKS = S // CHUNK
+SQUARE = 32
 F32 = mybir.dt.float32
 BF16 = mybir.dt.bfloat16
 I32 = mybir.dt.int32
@@ -23,7 +23,9 @@ RELU = mybir.ActivationFunctionType.Relu
 ADD = mybir.AluOpType.add
 
 SCALAR_GROUPS = 64
+EARLY = 768
 ROW_START, ROW_STEP = 11, 7
+SCALES_AT = 4 * M - 64
 
 
 def tile_list_tabmlp_tm_bias_kernel(tc, tab, w1, w2_words, w2_scales, b, offs, out):
@@ -39,22 +41,32 @@ def tile_list_tabmlp_tm_bias_kernel(tc, tab, w1, w2_words, w2_scales, b, offs, o
             return psum.tile([P, BANK], F32, name=f"bank{number}")
 
         offsets = keep.tile([P, S // 16], U16, name="offsets")
-        b_col = keep.tile([P, 8], F32, name="b_col")
+        b_rows = keep.tile([P, SQUARE], F32, name="b_rows", align_bytes=64)
         tab_words = keep.tile([P, T], U32, name="tab_words", align_bytes=64)
-        tab_scales = shared.tile([P, T], U8, name="tab_scales", align_bytes=64, offset=0)
+        tab_scales = shared.tile([P, T], U8, name="tab_scales", align_bytes=64, offset=SCALES_AT)
         w1_raw = keep.tile([P, 4, H], F32, name="w1_raw", tag="w1_raw", align_bytes=64)
         scales_dram = tab[0, 512 * T : 528 * T].rearrange("(q t) -> q t", q=16)
         words_dram = tab[0, 0 : 512 * T].rearrange("(p b) -> p b", p=P)
 
-        gathered_scales = keep.tile([P, S], U8, name="gathered_scales", align_bytes=64)
+        gathered_scales = keep.tile([P, S], U8, name="gathered_scales", tag="gathered_scales", align_bytes=64)
         x_scales = keep.tile([P, S], U8, name="x_scales", align_bytes=64)
         nc.vector.memset(tab_scales[:].bitcast(I32), 0)
         nc.vector.memset(x_scales[:].bitcast(I32), 0)
 
+        idle = keep.tile([P, 4 * BANK + BANK + 2 * P], U8, name="idle", align_bytes=64)
+        idle_codes = idle[:, : 4 * BANK].bitcast(U32)
+        idle_scales = idle[:, 4 * BANK : 5 * BANK]
+        zeros = idle[:, 5 * BANK :].bitcast(BF16)
+        nc.vector.memset(idle[:].bitcast(I32), 0)
+        nc.vector.quantize_mx(out=idle_codes[:, :SQUARE].bitcast(FP8X4), scales=idle_scales[:, :SQUARE], in_=zeros)
+
         w1_rows = w1.rearrange("(p j) r -> p j r", j=4)
-        nc.sync.dma_start(out=w1_raw[:, :1], in_=w1_rows[:, :1])
+        for quadrant in range(4):
+            queue = nc.sync if quadrant == 3 else nc.scalar
+            if quadrant == 1:
+                nc.sync.dma_start(out=w1_raw[:, :1], in_=w1_rows[:, :1])
+            queue.dma_start(out=b_rows[SQUARE * quadrant : SQUARE * (quadrant + 1), :], in_=b.rearrange("(i c) -> i c", c=SQUARE))
         nc.sync.dma_start(offsets[:], offs)
-        nc.sync.dma_start(out=b_col[:], in_=b.rearrange("(n c) -> n c", c=8))
         nc.sync.dma_start(out=tab_scales[ROW_START : ROW_START + 16 * ROW_STEP : ROW_STEP, :].bitcast(I32), in_=scales_dram.bitcast(I32))
         nc.sync.dma_start(out=w1_raw[:, 1:], in_=w1_rows[:, 1:])
         nc.sync.dma_start(out=tab_words[:].bitcast(I32), in_=words_dram.bitcast(I32))
@@ -67,45 +79,49 @@ def tile_list_tabmlp_tm_bias_kernel(tc, tab, w1, w2_words, w2_scales, b, offs, o
                 in_=gathered_scales[first : first + 12 * ROW_STEP + 1 : 4 * ROW_STEP, :].bitcast(I32),
             )
 
-        w2_codes = shared.tile([P, 2 * M], U8, name="w2_codes", align_bytes=64, offset=M)
-        w2_sc = shared.tile([P, M], U8, name="w2_sc", align_bytes=64, offset=0)
-        nc.vector.memset(w2_sc[:].bitcast(I32), 0)
+        w2_codes = shared.tile([P, 2 * M], U8, name="w2_codes", align_bytes=64, offset=SCALES_AT + T - 64)
+        w2_sc = shared.tile([P, M], U8, name="w2_sc", align_bytes=64, offset=SCALES_AT + 64)
         nc.sync.dma_start(out=w2_codes[:].bitcast(I32), in_=w2_words[0].bitcast(I32))
         for row in range(4):
             nc.sync.dma_start(out=w2_sc[row:P:32, :].bitcast(I32), in_=w2_scales[0, row:16:4, :].bitcast(I32))
 
-        ident = keep.tile([P, P], F32, name="ident")
-        make_identity(nc, ident[:])
-        bias_banks = [bank(0), bank(1)]
-        for u in range(2):
-            for c in range(4):
-                column = b_col[:, 4 * u + c : 4 * u + c + 1].to_broadcast([P, P])
-                nc.tensor.transpose(bias_banks[u][:, P * c : P * c + P], column, ident[:])
+        narrow_codes = shared.tile([P, SQUARE], U32, name="narrow_codes", align_bytes=64, offset=SCALES_AT + 64 + M)
+        narrow_scales = shared.tile([P, SQUARE], U8, name="narrow_scales", align_bytes=64, offset=SCALES_AT + 64 + M + 4 * SQUARE)
+        nc.vector.quantize_mx(out=narrow_codes[:].bitcast(FP8X4), scales=narrow_scales[:], in_=zeros)
+        for number in (0, 1, 6, 7):
+            nc.tensor.matmul_mx(
+                out=bank(number)[:SQUARE, :],
+                lhsT=narrow_codes[:].bitcast(FP8X4),
+                lhsT_scale=narrow_scales[:],
+                rhs=idle_codes.bitcast(FP8X4),
+                rhs_scale=idle_scales,
+                start=True,
+                stop=True,
+            )
 
-        w1_bf = keep.tile([P, 4 * H], BF16, name="w1_bf", align_bytes=64)
+        b_cols = keep.tile([P, SQUARE], F32, name="b_cols", align_bytes=64)
+        nc.vector.transpose(b_cols[:], b_rows[:])
+        bias = shared.tile([P, M], F32, name="bias", align_bytes=64, offset=0)
+
+        def widen(n0, n1, tag):
+            wide = keep.tile([P, n1 - n0], F32, name="b_wide", tag=tag, align_bytes=64)
+            source = b_cols[:, n0 // SQUARE : n1 // SQUARE].unsqueeze(2).to_broadcast([P, (n1 - n0) // SQUARE, SQUARE])
+            nc.scalar.activation(wide[:].rearrange("p (c a) -> p c a", a=SQUARE), source, COPY)
+            return wide
+
+        early = widen(0, EARLY, "early")
+        nc.vector.transpose(bias[:, :256], early[:, :256])
+
+        w1_bf = keep.tile([P, 4 * H], BF16, name="w1_bf", tag="w1_bf", align_bytes=64)
         w1_dst = w1_bf[:].rearrange("p (t m j) -> p m t j", t=4, j=4)
         w1_src = w1_raw[:].rearrange("p j (m t) -> p m t j", t=4)
         for rows in (slice(0, 1), slice(1, 4)):
             nc.scalar.activation(w1_dst[:, :SCALAR_GROUPS, :, rows], w1_src[:, :SCALAR_GROUPS, :, rows], COPY)
         nc.vector.tensor_copy(out=w1_dst[:, SCALAR_GROUPS:], in_=w1_src[:, SCALAR_GROUPS:])
+        nc.vector.transpose(bias[:, 256:EARLY], early[:, 256:])
         w1_codes = keep.tile([P, H], U32, name="w1_codes", align_bytes=64)
         w1_sc = keep.tile([P, H], U8, name="w1_sc", align_bytes=64)
         nc.vector.quantize_mx(out=w1_codes[:].bitcast(FP8X4), scales=w1_sc[:], in_=w1_bf[:])
-
-        bias = keep.tile([P, M], F32, name="bias", tag="w1_raw", align_bytes=64)
-        bias_v = bias[:].rearrange("p (n u c) -> p u n c", u=2, c=4)
-        for u in range(2):
-            nc.scalar.activation(bias_v[:, u], bias_banks[u][:].rearrange("p (c n) -> p n c", c=4), COPY)
-
-        nc.tensor.matmul_mx(
-            out=bank(0)[:],
-            lhsT=w1_codes[:, :P].bitcast(FP8X4),
-            lhsT_scale=w1_sc[:, :P],
-            rhs=w1_codes[:].bitcast(FP8X4),
-            rhs_scale=w1_sc[:],
-            start=True,
-            stop=True,
-        )
 
         h_rounded = [ring.tile([P, 4 * CHUNK], BF16, name="h_bf", align_bytes=64) for chunk in range(CHUNKS)]
         h_codes = []
@@ -174,7 +190,10 @@ def tile_list_tabmlp_tm_bias_kernel(tc, tab, w1, w2_words, w2_scales, b, offs, o
                 done = done + width
             nc.sync.dma_start(out=out[CHUNK * chunk : CHUNK * chunk + CHUNK, n0 : n0 + total], in_=result[:, :total])
 
-        x_words = [look_up(chunk) for chunk in range(CHUNKS)]
+        late = widen(EARLY, M, "gathered_scales")
+        x_words = [look_up(chunk) for chunk in range(CHUNKS - 1)]
+        nc.vector.transpose(bias[:, EARLY:], late[:])
+        x_words.append(look_up(CHUNKS - 1))
 
         first_product(0, bank(2))
         first_product(1, bank(3))

@@ -21,9 +21,9 @@ FP4X4 = mybir.dt.float4_e2m1fn_x4
 COPY = mybir.ActivationFunctionType.Copy
 RELU = mybir.ActivationFunctionType.Relu
 ADD = mybir.AluOpType.add
+MULT = mybir.AluOpType.mult
 
-SCALAR_GROUPS = 64
-EARLY = 768
+SCALAR_GROUPS = 72
 ROW_START, ROW_STEP = 11, 7
 SCALES_AT = 4 * M - 64
 
@@ -33,6 +33,7 @@ def tile_list_tabmlp_tm_bias_kernel(tc, tab, w1, w2_words, w2_scales, b, offs, o
     with ExitStack() as ctx:
         keep = ctx.enter_context(tc.tile_pool(name="keep", bufs=1))
         shared = ctx.enter_context(tc.tile_pool(name="shared", bufs=1))
+        turns = ctx.enter_context(tc.tile_pool(name="turns", bufs=1))
         ring = ctx.enter_context(tc.tile_pool(name="ring", bufs=CHUNKS))
         outs = ctx.enter_context(tc.tile_pool(name="outs", bufs=10))
         psum = ctx.enter_context(tc.psum_pool(name="psum", bufs=1))
@@ -44,11 +45,12 @@ def tile_list_tabmlp_tm_bias_kernel(tc, tab, w1, w2_words, w2_scales, b, offs, o
         b_rows = keep.tile([P, SQUARE], F32, name="b_rows", align_bytes=64)
         tab_words = keep.tile([P, T], U32, name="tab_words", align_bytes=64)
         tab_scales = shared.tile([P, T], U8, name="tab_scales", align_bytes=64, offset=SCALES_AT)
-        w1_raw = keep.tile([P, 4, H], F32, name="w1_raw", tag="w1_raw", align_bytes=64)
+        w1_flat = turns.tile([P, 4 * H], F32, name="w1_flat", align_bytes=64, offset=0)
+        w1_raw = w1_flat[:].rearrange("p (j r) -> p j r", j=4)
         scales_dram = tab[0, 512 * T : 528 * T].rearrange("(q t) -> q t", q=16)
         words_dram = tab[0, 0 : 512 * T].rearrange("(p b) -> p b", p=P)
 
-        gathered_scales = keep.tile([P, S], U8, name="gathered_scales", tag="gathered_scales", align_bytes=64)
+        gathered_scales = keep.tile([P, S], U8, name="gathered_scales", align_bytes=64)
         x_scales = keep.tile([P, S], U8, name="x_scales", align_bytes=64)
         nc.vector.memset(tab_scales[:].bitcast(I32), 0)
         nc.vector.memset(x_scales[:].bitcast(I32), 0)
@@ -60,23 +62,23 @@ def tile_list_tabmlp_tm_bias_kernel(tc, tab, w1, w2_words, w2_scales, b, offs, o
         nc.vector.memset(idle[:].bitcast(I32), 0)
         nc.vector.quantize_mx(out=idle_codes[:, :SQUARE].bitcast(FP8X4), scales=idle_scales[:, :SQUARE], in_=zeros)
 
-        w1_rows = w1.rearrange("(p j) r -> p j r", j=4)
+        w1_rows = w1.rearrange("(p j) r -> p (j r)", j=4)
         for quadrant in range(4):
             queue = nc.sync if quadrant == 3 else nc.scalar
             if quadrant == 1:
-                nc.sync.dma_start(out=w1_raw[:, :1], in_=w1_rows[:, :1])
+                nc.sync.dma_start(out=w1_flat[:, :H], in_=w1_rows[:, :H])
             queue.dma_start(out=b_rows[SQUARE * quadrant : SQUARE * (quadrant + 1), :], in_=b.rearrange("(i c) -> i c", c=SQUARE))
         nc.sync.dma_start(offsets[:], offs)
         nc.sync.dma_start(out=tab_scales[ROW_START : ROW_START + 16 * ROW_STEP : ROW_STEP, :].bitcast(I32), in_=scales_dram.bitcast(I32))
-        nc.sync.dma_start(out=w1_raw[:, 1:], in_=w1_rows[:, 1:])
+        nc.sync.dma_start(out=w1_flat[:, H:], in_=w1_rows[:, H:])
         nc.sync.dma_start(out=tab_words[:].bitcast(I32), in_=words_dram.bitcast(I32))
 
         nc.vector.tensor_copy(gathered_scales[:], tab_scales[:].indirect(offsets[:]))
         for row in range(4):
-            first = ROW_START + ROW_STEP * row
+            lowest = ROW_START + ROW_STEP * row
             nc.sync.dma_start(
                 out=x_scales[row:P:32, :].bitcast(I32),
-                in_=gathered_scales[first : first + 12 * ROW_STEP + 1 : 4 * ROW_STEP, :].bitcast(I32),
+                in_=gathered_scales[lowest : lowest + 12 * ROW_STEP + 1 : 4 * ROW_STEP, :].bitcast(I32),
             )
 
         w2_codes = shared.tile([P, 2 * M], U8, name="w2_codes", align_bytes=64, offset=SCALES_AT + T - 64)
@@ -109,16 +111,15 @@ def tile_list_tabmlp_tm_bias_kernel(tc, tab, w1, w2_words, w2_scales, b, offs, o
             nc.scalar.activation(wide[:].rearrange("p (c a) -> p c a", a=SQUARE), source, COPY)
             return wide
 
-        early = widen(0, EARLY, "early")
-        nc.vector.transpose(bias[:, :256], early[:, :256])
+        for n0 in (0, BANK):
+            nc.vector.transpose(bias[:, n0 : n0 + BANK], widen(n0, n0 + BANK, f"wide{n0}")[:])
 
-        w1_bf = keep.tile([P, 4 * H], BF16, name="w1_bf", tag="w1_bf", align_bytes=64)
+        w1_bf = keep.tile([P, 4 * H], BF16, name="w1_bf", align_bytes=64)
         w1_dst = w1_bf[:].rearrange("p (t m j) -> p m t j", t=4, j=4)
-        w1_src = w1_raw[:].rearrange("p j (m t) -> p m t j", t=4)
+        w1_src = w1_raw.rearrange("p j (m t) -> p m t j", t=4)
         for rows in (slice(0, 1), slice(1, 4)):
             nc.scalar.activation(w1_dst[:, :SCALAR_GROUPS, :, rows], w1_src[:, :SCALAR_GROUPS, :, rows], COPY)
-        nc.vector.tensor_copy(out=w1_dst[:, SCALAR_GROUPS:], in_=w1_src[:, SCALAR_GROUPS:])
-        nc.vector.transpose(bias[:, 256:EARLY], early[:, 256:])
+        nc.gpsimd.tensor_scalar(w1_dst[:, SCALAR_GROUPS:], w1_src[:, SCALAR_GROUPS:], 1.0, 0.0, MULT, ADD)
         w1_codes = keep.tile([P, H], U32, name="w1_codes", align_bytes=64)
         w1_sc = keep.tile([P, H], U8, name="w1_sc", align_bytes=64)
         nc.vector.quantize_mx(out=w1_codes[:].bitcast(FP8X4), scales=w1_sc[:], in_=w1_bf[:])
@@ -132,7 +133,7 @@ def tile_list_tabmlp_tm_bias_kernel(tc, tab, w1, w2_words, w2_scales, b, offs, o
             return [slice(0, CHUNK)]
 
         def look_up(chunk):
-            words = ring.tile([P, CHUNK], U32, name="x_words", align_bytes=64)
+            words = turns.tile([P, CHUNK], U32, name=f"x_words{chunk}", align_bytes=64, offset=4 * CHUNK * chunk)
             columns = slice(CHUNK // 16 * chunk, CHUNK // 16 * (chunk + 1))
             nc.vector.tensor_copy(words[:], tab_words[:].indirect(offsets[:, columns]))
             return words
@@ -190,10 +191,7 @@ def tile_list_tabmlp_tm_bias_kernel(tc, tab, w1, w2_words, w2_scales, b, offs, o
                 done = done + width
             nc.sync.dma_start(out=out[CHUNK * chunk : CHUNK * chunk + CHUNK, n0 : n0 + total], in_=result[:, :total])
 
-        late = widen(EARLY, M, "gathered_scales")
-        x_words = [look_up(chunk) for chunk in range(CHUNKS - 1)]
-        nc.vector.transpose(bias[:, EARLY:], late[:])
-        x_words.append(look_up(CHUNKS - 1))
+        x_words = [look_up(chunk) for chunk in range(CHUNKS)]
 
         first_product(0, bank(2))
         first_product(1, bank(3))

@@ -42,7 +42,7 @@ def tile_list_tabmlp_tm_bias_kernel(tc, tab, w1, w2_words, w2_scales, b, offs, o
             return psum.tile([P, BANK], F32, name=f"bank{number}")
 
         offsets = keep.tile([P, S // 16], U16, name="offsets")
-        b_rows = keep.tile([P, SQUARE], F32, name="b_rows", align_bytes=64)
+        b_rows = keep.tile([P, P], F32, name="b_rows", align_bytes=64)
         tab_words = keep.tile([P, T], U32, name="tab_words", align_bytes=64)
         tab_scales = shared.tile([P, T], U8, name="tab_scales", align_bytes=64, offset=SCALES_AT)
         w1_flat = turns.tile([P, 4 * H], F32, name="w1_flat", align_bytes=64, offset=0)
@@ -52,6 +52,7 @@ def tile_list_tabmlp_tm_bias_kernel(tc, tab, w1, w2_words, w2_scales, b, offs, o
 
         gathered_scales = keep.tile([P, S], U8, name="gathered_scales", align_bytes=64)
         x_scales = keep.tile([P, S], U8, name="x_scales", align_bytes=64)
+        nc.vector.memset(b_rows[:], 0.0)
         nc.vector.memset(tab_scales[:].bitcast(I32), 0)
         nc.vector.memset(x_scales[:].bitcast(I32), 0)
 
@@ -63,12 +64,9 @@ def tile_list_tabmlp_tm_bias_kernel(tc, tab, w1, w2_words, w2_scales, b, offs, o
         nc.vector.quantize_mx(out=idle_codes[:, :SQUARE].bitcast(FP8X4), scales=idle_scales[:, :SQUARE], in_=zeros)
 
         w1_rows = w1.rearrange("(p j) r -> p (j r)", j=4)
-        for quadrant in range(4):
-            queue = nc.sync if quadrant == 3 else nc.scalar
-            if quadrant == 1:
-                nc.sync.dma_start(out=w1_flat[:, :H], in_=w1_rows[:, :H])
-            queue.dma_start(out=b_rows[SQUARE * quadrant : SQUARE * (quadrant + 1), :], in_=b.rearrange("(i c) -> i c", c=SQUARE))
+        nc.sync.dma_start(out=w1_flat[:, :H], in_=w1_rows[:, :H])
         nc.sync.dma_start(offsets[:], offs)
+        nc.sync.dma_start(out=b_rows[0:P:4, :], in_=b.rearrange("(u c) -> u c", c=P).unsqueeze(0).to_broadcast([4, 8, P]))
         nc.sync.dma_start(out=tab_scales[ROW_START : ROW_START + 16 * ROW_STEP : ROW_STEP, :].bitcast(I32), in_=scales_dram.bitcast(I32))
         nc.sync.dma_start(out=w1_flat[:, H:], in_=w1_rows[:, H:])
         nc.sync.dma_start(out=tab_words[:].bitcast(I32), in_=words_dram.bitcast(I32))
@@ -101,14 +99,15 @@ def tile_list_tabmlp_tm_bias_kernel(tc, tab, w1, w2_words, w2_scales, b, offs, o
                 stop=True,
             )
 
-        b_cols = keep.tile([P, SQUARE], F32, name="b_cols", align_bytes=64)
+        b_cols = keep.tile([P, P], F32, name="b_cols", align_bytes=64)
         nc.vector.transpose(b_cols[:], b_rows[:])
         bias = shared.tile([P, M], F32, name="bias", align_bytes=64, offset=0)
 
         def widen(n0, n1, tag):
             wide = keep.tile([P, n1 - n0], F32, name="b_wide", tag=tag, align_bytes=64)
-            source = b_cols[:, n0 // SQUARE : n1 // SQUARE].unsqueeze(2).to_broadcast([P, (n1 - n0) // SQUARE, SQUARE])
-            nc.scalar.activation(wide[:].rearrange("p (c a) -> p c a", a=SQUARE), source, COPY)
+            source = b_cols[:].rearrange("p (c u s) -> p u c s", c=4, s=4)[:, n0 // P : n1 // P, :, 0:1]
+            source = source.to_broadcast([P, (n1 - n0) // P, 4, SQUARE])
+            nc.scalar.activation(wide[:].rearrange("p (u c a) -> p u c a", c=4, a=SQUARE), source, COPY)
             return wide
 
         for n0 in (0, BANK):

@@ -23,9 +23,9 @@ RELU = mybir.ActivationFunctionType.Relu
 ADD = mybir.AluOpType.add
 MULT = mybir.AluOpType.mult
 
-SCALAR_GROUPS = 72
+SCALAR_GROUPS = 64
+FIRST = 768
 ROW_START, ROW_STEP = 11, 7
-SCALES_AT = 4 * M - 64
 
 
 def tile_list_tabmlp_tm_bias_kernel(tc, tab, w1, w2_words, w2_scales, b, offs, out):
@@ -42,9 +42,9 @@ def tile_list_tabmlp_tm_bias_kernel(tc, tab, w1, w2_words, w2_scales, b, offs, o
             return psum.tile([P, BANK], F32, name=f"bank{number}")
 
         offsets = keep.tile([P, S // 16], U16, name="offsets")
-        b_rows = keep.tile([P, P], F32, name="b_rows", align_bytes=64)
+        b_rows = keep.tile([P, P], F32, name="b_rows", tag="b_rows", align_bytes=64)
         tab_words = keep.tile([P, T], U32, name="tab_words", align_bytes=64)
-        tab_scales = shared.tile([P, T], U8, name="tab_scales", align_bytes=64, offset=SCALES_AT)
+        tab_scales = shared.tile([P, T], U8, name="tab_scales", align_bytes=64, offset=0)
         w1_flat = turns.tile([P, 4 * H], F32, name="w1_flat", align_bytes=64, offset=0)
         w1_raw = w1_flat[:].rearrange("p (j r) -> p j r", j=4)
         scales_dram = tab[0, 512 * T : 528 * T].rearrange("(q t) -> q t", q=16)
@@ -79,29 +79,15 @@ def tile_list_tabmlp_tm_bias_kernel(tc, tab, w1, w2_words, w2_scales, b, offs, o
                 in_=gathered_scales[lowest : lowest + 12 * ROW_STEP + 1 : 4 * ROW_STEP, :].bitcast(I32),
             )
 
-        w2_codes = shared.tile([P, 2 * M], U8, name="w2_codes", align_bytes=64, offset=SCALES_AT + T - 64)
-        w2_sc = shared.tile([P, M], U8, name="w2_sc", align_bytes=64, offset=SCALES_AT + 64)
+        w2_codes = shared.tile([P, 2 * M], U8, name="w2_codes", align_bytes=64, offset=M)
+        w2_sc = shared.tile([P, M], U8, name="w2_sc", align_bytes=64, offset=0)
         nc.sync.dma_start(out=w2_codes[:].bitcast(I32), in_=w2_words[0].bitcast(I32))
         for row in range(4):
             nc.sync.dma_start(out=w2_sc[row:P:32, :].bitcast(I32), in_=w2_scales[0, row:16:4, :].bitcast(I32))
 
-        narrow_codes = shared.tile([P, SQUARE], U32, name="narrow_codes", align_bytes=64, offset=SCALES_AT + 64 + M)
-        narrow_scales = shared.tile([P, SQUARE], U8, name="narrow_scales", align_bytes=64, offset=SCALES_AT + 64 + M + 4 * SQUARE)
-        nc.vector.quantize_mx(out=narrow_codes[:].bitcast(FP8X4), scales=narrow_scales[:], in_=zeros)
-        for number in (0, 1, 6, 7):
-            nc.tensor.matmul_mx(
-                out=bank(number)[:SQUARE, :],
-                lhsT=narrow_codes[:].bitcast(FP8X4),
-                lhsT_scale=narrow_scales[:],
-                rhs=idle_codes.bitcast(FP8X4),
-                rhs_scale=idle_scales,
-                start=True,
-                stop=True,
-            )
-
         b_cols = keep.tile([P, P], F32, name="b_cols", align_bytes=64)
         nc.vector.transpose(b_cols[:], b_rows[:])
-        bias = shared.tile([P, M], F32, name="bias", align_bytes=64, offset=0)
+        bias = keep.tile([P, M], F32, name="bias", align_bytes=64)
 
         def widen(n0, n1, tag):
             wide = keep.tile([P, n1 - n0], F32, name="b_wide", tag=tag, align_bytes=64)
@@ -110,15 +96,29 @@ def tile_list_tabmlp_tm_bias_kernel(tc, tab, w1, w2_words, w2_scales, b, offs, o
             nc.scalar.activation(wide[:].rearrange("p (u c a) -> p u c a", c=4, a=SQUARE), source, COPY)
             return wide
 
-        for n0 in (0, BANK):
-            nc.vector.transpose(bias[:, n0 : n0 + BANK], widen(n0, n0 + BANK, f"wide{n0}")[:])
+        nc.vector.transpose(bias[:, :FIRST], widen(0, FIRST, "wide_low")[:])
+
+        narrow_codes = keep.tile([P, SQUARE], U32, name="narrow_codes", tag="b_rows", align_bytes=64)
+        nc.scalar.copy(narrow_codes[:], idle_codes[:, :SQUARE])
+        for number in (0, 1, 6, 7):
+            nc.tensor.matmul_mx(
+                out=bank(number)[:SQUARE, :],
+                lhsT=narrow_codes[:].bitcast(FP8X4),
+                lhsT_scale=idle_scales[:, :SQUARE],
+                rhs=idle_codes.bitcast(FP8X4),
+                rhs_scale=idle_scales,
+                start=True,
+                stop=True,
+            )
+
+        nc.vector.transpose(bias[:, FIRST:], widen(FIRST, M, "wide_high")[:])
 
         w1_bf = keep.tile([P, 4 * H], BF16, name="w1_bf", align_bytes=64)
         w1_dst = w1_bf[:].rearrange("p (t m j) -> p m t j", t=4, j=4)
         w1_src = w1_raw.rearrange("p j (m t) -> p m t j", t=4)
         for rows in (slice(0, 1), slice(1, 4)):
             nc.scalar.activation(w1_dst[:, :SCALAR_GROUPS, :, rows], w1_src[:, :SCALAR_GROUPS, :, rows], COPY)
-        nc.gpsimd.tensor_scalar(w1_dst[:, SCALAR_GROUPS:], w1_src[:, SCALAR_GROUPS:], 1.0, 0.0, MULT, ADD)
+            nc.gpsimd.tensor_scalar(w1_dst[:, SCALAR_GROUPS:, :, rows], w1_src[:, SCALAR_GROUPS:, :, rows], 1.0, 0.0, MULT, ADD)
         w1_codes = keep.tile([P, H], U32, name="w1_codes", align_bytes=64)
         w1_sc = keep.tile([P, H], U8, name="w1_sc", align_bytes=64)
         nc.vector.quantize_mx(out=w1_codes[:].bitcast(FP8X4), scales=w1_sc[:], in_=w1_bf[:])

from contextlib import ExitStack

import concourse.mybir as mybir

K, H, M, T, S = 512, 512, 1024, 2048, 512
FLOPS = 2 * K * H * S + 2 * H * M * S

P = 128
BANK = 512
CHUNK = 128
CHUNKS = S // CHUNK
SQUARE = 32
F32 = mybir.dt.float32
BF16 = mybir.dt.bfloat16
I32 = mybir.dt.int32
U32 = mybir.dt.uint32
U16 = mybir.dt.uint16
U8 = mybir.dt.uint8
FP8X4 = mybir.dt.float8_e4m3fn_x4
FP4X4 = mybir.dt.float4_e2m1fn_x4
COPY = mybir.ActivationFunctionType.Copy
RELU = mybir.ActivationFunctionType.Relu
ADD = mybir.AluOpType.add
MULT = mybir.AluOpType.mult

SCALAR_GROUPS = 64
FIRST = 768
ROW_START, ROW_STEP = 11, 7


def tile_list_tabmlp_tm_bias_kernel(tc, tab, w1, w2_words, w2_scales, b, offs, out):
    nc = tc.nc
    with ExitStack() as ctx:
        keep = ctx.enter_context(tc.tile_pool(name="keep", bufs=1))
        shared = ctx.enter_context(tc.tile_pool(name="shared", bufs=1))
        turns = ctx.enter_context(tc.tile_pool(name="turns", bufs=1))
        ring = ctx.enter_context(tc.tile_pool(name="ring", bufs=CHUNKS))
        outs = ctx.enter_context(tc.tile_pool(name="outs", bufs=10))
        psum = ctx.enter_context(tc.psum_pool(name="psum", bufs=1))

        def bank(number):
            return psum.tile([P, BANK], F32, name=f"bank{number}")

        offsets = keep.tile([P, S // 16], U16, name="offsets")
        b_rows = keep.tile([P, P], F32, name="b_rows", tag="b_rows", align_bytes=64)
        tab_words = keep.tile([P, T], U32, name="tab_words", align_bytes=64)
        tab_scales = shared.tile([P, T], U8, name="tab_scales", align_bytes=64, offset=0)
        w1_flat = turns.tile([P, 4 * H], F32, name="w1_flat", align_bytes=64, offset=0)
        w1_raw = w1_flat[:].rearrange("p (j r) -> p j r", j=4)
        scales_dram = tab[0, 512 * T : 528 * T].rearrange("(q t) -> q t", q=16)
        words_dram = tab[0, 0 : 512 * T].rearrange("(p b) -> p b", p=P)

        gathered_scales = keep.tile([P, S], U8, name="gathered_scales", align_bytes=64)
        x_scales = keep.tile([P, S], U8, name="x_scales", align_bytes=64)
        nc.vector.memset(b_rows[:], 0.0)
        nc.vector.memset(tab_scales[:].bitcast(I32), 0)
        nc.vector.memset(x_scales[:].bitcast(I32), 0)

        idle = keep.tile([P, 4 * BANK + BANK + 2 * P], U8, name="idle", align_bytes=64)
        idle_codes = idle[:, : 4 * BANK].bitcast(U32)
        idle_scales = idle[:, 4 * BANK : 5 * BANK]
        zeros = idle[:, 5 * BANK :].bitcast(BF16)
        nc.vector.memset(idle[:].bitcast(I32), 0)
        nc.vector.quantize_mx(out=idle_codes[:, :SQUARE].bitcast(FP8X4), scales=idle_scales[:, :SQUARE], in_=zeros)

        w1_rows = w1.rearrange("(p j) r -> p (j r)", j=4)
        nc.sync.dma_start(out=w1_flat[:, :H], in_=w1_rows[:, :H])
        nc.sync.dma_start(offsets[:], offs)
        nc.sync.dma_start(out=b_rows[0:P:4, :], in_=b.rearrange("(u c) -> u c", c=P).unsqueeze(0).to_broadcast([4, 8, P]))
        nc.sync.dma_start(out=tab_scales[ROW_START : ROW_START + 16 * ROW_STEP : ROW_STEP, :].bitcast(I32), in_=scales_dram.bitcast(I32))
        nc.sync.dma_start(out=w1_flat[:, H:], in_=w1_rows[:, H:])
        nc.sync.dma_start(out=tab_words[:].bitcast(I32), in_=words_dram.bitcast(I32))

        nc.vector.tensor_copy(gathered_scales[:], tab_scales[:].indirect(offsets[:]))
        for row in range(4):
            lowest = ROW_START + ROW_STEP * row
            nc.sync.dma_start(
                out=x_scales[row:P:32, :].bitcast(I32),
                in_=gathered_scales[lowest : lowest + 12 * ROW_STEP + 1 : 4 * ROW_STEP, :].bitcast(I32),
            )

        w2_codes = shared.tile([P, 2 * M], U8, name="w2_codes", align_bytes=64, offset=M)
        w2_sc = shared.tile([P, M], U8, name="w2_sc", align_bytes=64, offset=0)
        nc.sync.dma_start(out=w2_codes[:].bitcast(I32), in_=w2_words[0].bitcast(I32))
        for row in range(4):
            nc.sync.dma_start(out=w2_sc[row:P:32, :].bitcast(I32), in_=w2_scales[0, row:16:4, :].bitcast(I32))

        b_cols = keep.tile([P, P], F32, name="b_cols", align_bytes=64)
        nc.vector.transpose(b_cols[:], b_rows[:])
        bias = keep.tile([P, M], F32, name="bias", align_bytes=64)

        def widen(n0, n1, tag):
            wide = keep.tile([P, n1 - n0], F32, name="b_wide", tag=tag, align_bytes=64)
            source = b_cols[:].rearrange("p (c u s) -> p u c s", c=4, s=4)[:, n0 // P : n1 // P, :, 0:1]
            source = source.to_broadcast([P, (n1 - n0) // P, 4, SQUARE])
            nc.scalar.activation(wide[:].rearrange("p (u c a) -> p u c a", c=4, a=SQUARE), source, COPY)
            return wide

        nc.vector.transpose(bias[:, :FIRST], widen(0, FIRST, "wide_low")[:])

        narrow_codes = keep.tile([P, SQUARE], U32, name="narrow_codes", tag="b_rows", align_bytes=64)
        nc.scalar.copy(narrow_codes[:], idle_codes[:, :SQUARE])
        for number in (0, 1, 6, 7):
            nc.tensor.matmul_mx(
                out=bank(number)[:SQUARE, :],
                lhsT=narrow_codes[:].bitcast(FP8X4),
                lhsT_scale=idle_scales[:, :SQUARE],
                rhs=idle_codes.bitcast(FP8X4),
                rhs_scale=idle_scales,
                start=True,
                stop=True,
            )

        nc.vector.transpose(bias[:, FIRST:], widen(FIRST, M, "wide_high")[:])

        w1_bf = keep.tile([P, 4 * H], BF16, name="w1_bf", align_bytes=64)
        w1_dst = w1_bf[:].rearrange("p (t m j) -> p m t j", t=4, j=4)
        w1_src = w1_raw.rearrange("p j (m t) -> p m t j", t=4)
        for rows in (slice(0, 1), slice(1, 4)):
            nc.scalar.activation(w1_dst[:, :SCALAR_GROUPS, :, rows], w1_src[:, :SCALAR_GROUPS, :, rows], COPY)
            nc.gpsimd.tensor_scalar(w1_dst[:, SCALAR_GROUPS:, :, rows], w1_src[:, SCALAR_GROUPS:, :, rows], 1.0, 0.0, MULT, ADD)
        w1_codes = keep.tile([P, H], U32, name="w1_codes", align_bytes=64)
        w1_sc = keep.tile([P, H], U8, name="w1_sc", align_bytes=64)
        nc.vector.quantize_mx(out=w1_codes[:].bitcast(FP8X4), scales=w1_sc[:], in_=w1_bf[:])

        h_rounded = [ring.tile([P, 4 * CHUNK], BF16, name="h_bf", align_bytes=64) for chunk in range(CHUNKS)]
        h_codes = []

        def parts(chunk):
            if chunk < 2:
                return [slice(0, CHUNK // 2), slice(CHUNK // 2, CHUNK)]
            return [slice(0, CHUNK)]

        def look_up(chunk):
            words = turns.tile([P, CHUNK], U32, name=f"x_words{chunk}", align_bytes=64, offset=4 * CHUNK * chunk)
            columns = slice(CHUNK // 16 * chunk, CHUNK // 16 * (chunk + 1))
            nc.vector.tensor_copy(words[:], tab_words[:].indirect(offsets[:, columns]))
            return words

        def first_product(chunk, h_bank, planes=range(4)):
            for place, t in enumerate(planes):
                quarter = slice(P * t, P * t + P)
                nc.tensor.matmul_mx(
                    out=h_bank[:, P * place : P * place + P],
                    lhsT=w1_codes[:, quarter].bitcast(FP8X4),
                    lhsT_scale=w1_sc[:, quarter],
                    rhs=x_words[chunk][:].bitcast(FP8X4),
                    rhs_scale=x_scales[:, CHUNK * chunk : CHUNK * chunk + CHUNK],
                    start=True,
                    stop=True,
                )
            dst = h_rounded[chunk][:].rearrange("p (n t) -> p n t", t=4)[:, :, planes.start : planes.stop]
            src = h_bank[:, : P * len(planes)].rearrange("p (t n) -> p n t", t=len(planes))
            for part in parts(chunk):
                nc.scalar.activation(dst[:, part], src[:, part], RELU)

        def quantise(chunk):
            codes = ring.tile([P, CHUNK], U32, name="h_codes", align_bytes=64, bufs=2)
            scales = ring.tile([P, CHUNK], U8, name="h_scales", align_bytes=64, bufs=2)
            for part in parts(chunk):
                nc.vector.quantize_mx(
                    out=codes[:, part].bitcast(FP8X4),
                    scales=scales[:, part],
                    in_=h_rounded[chunk][:, 4 * part.start : 4 * part.stop],
                )
            h_codes.append((codes, scales))

        def second_pass(chunk, n0, width, y_bank):
            codes, scales = h_codes[chunk]
            nc.tensor.matmul_mx(
                out=y_bank[:, :width],
                lhsT=codes[:].bitcast(FP8X4),
                lhsT_scale=scales[:],
                rhs=w2_codes[:, 2 * n0 : 2 * (n0 + width)].bitcast(FP4X4),
                rhs_scale=w2_sc[:, n0 : n0 + width],
                start=True,
                stop=True,
            )
            return y_bank[:, :width]

        def block(chunk, n0, width, y_bank, result):
            nc.vector.tensor_tensor(result, second_pass(chunk, n0, width, y_bank), bias[:, n0 : n0 + width], ADD)

        def blocks(chunk, n0, *pieces):
            total = sum(width for width, y_bank in pieces)
            result = outs.tile([P, BANK], F32, name="result")
            done = 0
            for width, y_bank in pieces:
                block(chunk, n0 + done, width, y_bank, result[:, done : done + width])
                done = done + width
            nc.sync.dma_start(out=out[CHUNK * chunk : CHUNK * chunk + CHUNK, n0 : n0 + total], in_=result[:, :total])

        x_words = [look_up(chunk) for chunk in range(CHUNKS)]

        first_product(0, bank(2))
        first_product(1, bank(3))
        first_product(2, bank(4), range(2))
        quantise(0)
        quantise(1)
        blocks(0, 0, (128, bank(5)))
        blocks(0, 128, (128, bank(6)), (256, bank(7)))
        blocks(0, BANK, (256, bank(0)), (256, bank(1)))
        first_product(2, bank(5), range(2, 4))
        blocks(1, 0, (BANK, bank(2)))
        first_product(3, bank(6))
        quantise(2)
        blocks(1, BANK, (BANK, bank(7)))
        quantise(3)
        blocks(2, 0, (256, bank(3)), (256, bank(4)))
        blocks(2, BANK, (BANK, bank(5)))
        blocks(3, 0, (BANK, bank(0)))
        blocks(3, BANK, (BANK, bank(1)))
